import numpy as np, ml_dtypes
CORES = [8,136,40,168]
N = 4
BF = ml_dtypes.bfloat16
def gentries(a):
    return np.ascontiguousarray(a.reshape(8, 16, -1).transpose(0, 2, 1)).reshape(8, -1)
def gtable(e):
    e = np.asarray(e); return np.ascontiguousarray(e.reshape(8, -1, 16).transpose(0, 2, 1)).reshape(128, -1).astype(np.int32)
def f(rng, *shape):
    return (rng.standard_normal(shape, dtype=np.float32) * np.exp2(rng.integers(-2, 3, shape[:-1] + (1,)))).astype(BF)
def wide(rng, *shape):
    v = f(rng, *shape).astype(np.float32); k = shape[:-2] + (1, shape[-1])
    return (v * np.exp2(rng.integers(-6, 7, k)) * (rng.random(k) > 0.0625)).astype(BF)
M, S, D, Q = 2048, 64, 8, 2
P = N // Q
def forest(rng, L, aside, bushy, zero=False):
    free = S + rng.permutation(M - S); n = S * (D - 1)
    chain = np.concatenate([np.arange(S)[:, None], free[:n].reshape(S, D - 1)], 1)
    p = np.arange(M); dep = np.full(M, -1); dep[chain] = np.arange(D); p[chain[:, 1:]] = chain[:, :-1]; rest = free[n:]
    if bushy:
        h = len(rest) // 2; p[rest[:h]] = rng.integers(0, S); p[rest[h:]] = chain[rng.integers(0, S), D - 2]
    else:
        lev = rng.integers(1, D, len(rest))
        for d in range(1, D):
            v = rest[lev == d]; p[v] = rng.choice(np.flatnonzero(dep == d - 1), len(v)); dep[v] = d
    kids = S + rng.permutation(M - S); o = kids[np.argsort(p[kids], kind="stable")]; q = p[o]
    sib = np.zeros(M, np.int64); sib[o] = np.arange(M - S) - np.searchsorted(q, q); c = np.bincount(q, minlength=M)
    base = rng.integers(0, 4096, M); step = 2 * rng.integers(0, 2048, M) + 1
    if zero: base[0] = 0
    x = np.where((c > 0) & (rng.random(M) < 0.7), (rng.random(M) * c).astype(np.int64), c + (rng.random(M) * (4096 - c)).astype(np.int64))
    x[chain[:, :-1]] = sib[chain[:, 1:]]
    e = np.flatnonzero(L < D - 1); b = chain[e, L[e]]; w = sib[chain[e, L[e] + 1]]; cb = c[b]
    other = (w + 1 + (rng.random(len(e)) * (cb - 1)).astype(np.int64)) % cb; none = cb + (rng.random(len(e)) * (4096 - cb)).astype(np.int64)
    x[b] = np.where((cb > 1) & (rng.random(len(e)) < aside), other, none)
    t = (base + step * x) % 4096
    k = np.zeros(M, np.int64); k[o] = (base[q] + step[q] * sib[o]) % 4096
    k[:S] = np.where(rng.random(S) < 0.5, t[:S], rng.integers(0, 4096, S))
    return p, k, t
def shards(rng, t, sc, tie):
    v = sc * 4096 + t; win = rng.integers(0, N, t.shape); u = rng.random((N,) + t.shape)
    o = np.where(rng.random(t.shape) < tie, sc * 4096 + (u * (t + 1)).astype(np.int64), (u * (v + 1)).astype(np.int64))
    o = np.where((np.arange(N)[:, None, None, None] == win) | (rng.random(o.shape) < 0.03125), v, np.minimum(o, v))
    return np.ascontiguousarray(o.transpose(0, 2, 1, 3)).reshape(N, 8, N * M).astype(np.int32)
def draw(rng, L, aside=0.5, bushy=False, tie=0.125, uneven=False, zero=False):
    a = [[forest(rng, L[q, g], aside, bushy, zero) for g in range(8)] for q in range(N)]
    p, k, t = [np.array([[a[q][g][i] for g in range(8)] for q in range(N)]) for i in range(3)]
    sc = rng.integers(0, 4096, t.shape)
    if uneven: sc = 4095 >> rng.integers(0, 13, t.shape)
    return {"par": np.stack([gtable(p[q]) for q in range(N)]), "tok": k.astype(np.int32), "best": shards(rng, t, sc, tie), "kv": f(rng, N, 128, Q * M)}
def setup_inputs(rng):
    return draw(rng, rng.integers(0, D, (N, 8, S)))
def setup_inputs_full(rng):
    return draw(rng, np.full((N, 8, S), D - 1))
def setup_inputs_cut(rng):
    return draw(rng, rng.choice(np.array([0, 1, D - 2]), (N, 8, S)), aside=0.0, zero=True)
def setup_inputs_ties(rng):
    return draw(rng, rng.integers(0, D, (N, 8, S)), tie=1.0)
def setup_inputs_bushy(rng):
    return draw(rng, rng.integers(0, D, (N, 8, S)), bushy=True)
def setup_inputs_spread(rng):
    d = draw(rng, rng.integers(0, D, (N, 8, S)), uneven=True); d["kv"] = wide(rng, N, 128, Q * M); return d
def check_inputs(d):
    bad = []; p = np.stack([gentries(a) for a in d["par"]]).astype(np.int64); k = d["tok"].astype(np.int64); b = d["best"]
    if not np.isfinite(d["kv"].astype(np.float32)).all(): bad.append("finite")
    if b.min() < 0 or b.max() >= 1 << 24: bad.append("best")
    if k.min() < 0 or k.max() > 4095: bad.append("tokens")
    if p.min() < 0 or p.max() >= M: return bad + ["parents"]
    if (p[:, :, :S] != np.arange(S)).any(): bad.append("roots")
    a = p
    for i in range(D - 2): a = np.take_along_axis(p, a, 2)
    if (a >= S).any(): bad.append("depth")
    w = np.sort((p * 4096 + k)[:, :, S:], axis=2)
    if (w[:, :, 1:] == w[:, :, :-1]).any(): bad.append("children")
    return bad
def reference(par, tok, best, kv):
    p = np.stack([gentries(a) for a in par]).astype(np.int64)
    t = np.max(best, axis=0).reshape(8, N, M).transpose(1, 0, 2) & 4095
    ok = (np.arange(M) < S) | (tok == np.take_along_axis(t, p, 2))
    a = np.broadcast_to(np.arange(M), p.shape); acc = np.ones(p.shape, bool); dep = np.zeros(p.shape, np.int64)
    for i in range(D):
        acc = acc & np.take_along_axis(ok, a, 2); dep = dep + (a >= S); a = np.take_along_axis(p, a, 2)
    y = np.zeros((N, 128, Q * S * D), BF)
    for r in range(N):
        out = y[r].reshape(8, 16, Q * S * D)
        for i in range(Q):
            q = P * i + r % P; k = kv[r][:, i * M:(i + 1) * M].reshape(8, 16, M)
            g, j = np.nonzero(acc[q])
            out[g, :, (i * S + a[q, g, j]) * D + dep[q, g, j]] = k[g, :, j]
    return {"y": y}

@@ -1,0 +1,266 @@
+from concourse.mybir import AluOpType as Op, ActivationFunctionType as Fn
+
+NA = 72
+C0, C1, C2 = 4, 4 + NA, 128
+NODE = 2048
+WIN = NODE + 2064
+
+SCRATCH = {
+    "own": ("sbuf", [128, 128], "int32"),
+    "snd": ("sbuf", [128, 384], "int32"),
+    "land1": ("sbuf", [128, 128], "int32"),
+    "land2": ("sbuf", [128, 128], "int32"),
+    "land3": ("sbuf", [128, 128], "int32"),
+    "mx": ("sbuf", [128, 384], "int32"),
+    "tgt": ("sbuf", [128, 128], "int32"),
+    "tokc": ("sbuf", [128, 128], "int32"),
+    "tokf": ("sbuf", [128, 128], "float16"),
+    "part": ("sbuf", [128, 128], "int32"),
+    "parlo": ("sbuf", [128, 128], "int32"),
+    "parhi": ("sbuf", [128, 128], "int32"),
+    "lo": ("sbuf", [128, 128], "uint16"),
+    "hi": ("sbuf", [128, 128], "uint16"),
+    "pcol": ("sbuf", [128, 128], "float32"),
+    "pid": ("sbuf", [128, 1], "int32"),
+    "pmi": ("sbuf", [128, 1], "int32"),
+    "pmod": ("sbuf", [128, 1], "float32"),
+    "mb": ("sbuf", [128, 128], "bfloat16"),
+    "ed": ("sbuf", [128, 128], "int32"),
+    "mbt": ("sbuf", [128, 128], "bfloat16"),
+    "d15": ("sbuf", [128, 64], "int32"),
+    "c16": ("sbuf", [128, 16], "float32"),
+    "neg": ("sbuf", [128, 64], "float32"),
+    "sel": ("sbuf", [128, 2048], "float16"),
+    "tab": ("sbuf", [128, 2048], "float16"),
+    "cst": ("sbuf", [128, 128], "bfloat16"),
+    "mmod": ("sbuf", [128, 128], "bfloat16"),
+    "c16r": ("sbuf", [128, 128], "bfloat16"),
+    "rst": ("sbuf", [128, 64], "float32"),
+    "yri": ("sbuf", [128, 64], "float32"),
+    "yr": ("sbuf", [128, 64], "float16"),
+    "ri": ("sbuf", [128, 4], "int32"),
+    "jrow": ("sbuf", [128, 1984], "float32"),
+    "tokrow": ("sbuf", [128, 2048], "float32"),
+    "tokx": ("sbuf", [128, 2048], "float32"),
+    "eq": ("sbuf", [128, 2048], "float16"),
+    "offi": ("sbuf", [128, 128], "float32"),
+    "off": ("sbuf", [128, 128], "uint16"),
+    "zero": ("sbuf", [128, 516], "float32"),
+    "wa": ("sbuf", [128, WIN], "float32"),
+    "wb": ("sbuf", [128, WIN], "float32"),
+    "xs": ("sbuf", [128, 448], "float32"),
+    "ys": ("sbuf", [128, 448], "float16"),
+    "ts": ("sbuf", [128, 448], "float32"),
+    "ls": ("sbuf", [128, 64], "uint16"),
+    "fl": ("sbuf", [128, 32], "uint16"),
+    "fl2": ("sbuf", [128, 32], "uint16"),
+    "kva": ("sbuf", [128, 2064], "bfloat16"),
+    "kvb": ("sbuf", [128, 2064], "bfloat16"),
+    "ya": ("sbuf", [128, 512], "bfloat16"),
+    "yb": ("sbuf", [128, 256], "bfloat16"),
+    "yc": ("sbuf", [128, 256], "bfloat16"),
+    "tr0": ("psum", [128, 512], "float32"),
+    "tr1": ("psum", [128, 512], "float32"),
+    "tr2": ("psum", [128, 512], "float32"),
+    "tr3": ("psum", [128, 512], "float32"),
+    "psa": ("psum", [128, 512], "float32"),
+    "psb": ("psum", [128, 512], "float32"),
+    "psf": ("psum", [128, 512], "float32"),
+}
+SEMAPHORES = (["ld1", "ld2", "ld3", "ldown", "ldtok", "ldpar", "ldkv", "sent", "arr1", "arr2", "arr3", "lst", "lsent", "st1", "st2",
+               "gpid", "gmb", "ged", "gpre", "grst", "gyr", "gri", "gj",
+               "vz", "vkz", "vcst", "vsel", "vtok", "vpar", "vlists", "vpmi", "vpmod", "vmbt", "vtab", "vd15", "vc16", "vyr", "vl",
+               "vtx", "vm1", "vm2", "vm3", "vtgt", "veqa", "veqb", "voa", "vob", "voffa", "voffb", "vscb", "vfl", "vya", "vyb",
+               "afa", "afb", "ev0", "ev1", "ev2", "ev3", "asca", "ayc", "ptr0", "ptr1", "ptr2", "ptr3", "poka", "pokb", "pf"]
+              + ["x%d" % d for d in range(7)] + ["y%d" % d for d in range(7)] + ["t%d" % d for d in range(6)]
+              + ["l%d" % d for d in range(6)])
+
+
+def rank_program(g, core, T, topo):
+    r = T.rank_of(core)
+    if r is None:
+        return
+    S = T.sem
+    cores = T.cores
+    n = len(cores)
+    V, A, P, Y = g.vector, g.scalar, g.tensor, g.sync
+    mate = (r + 2) % n
+    mine, other = r // 2, 1 - r // 2
+
+    def blk(q):
+        return T.best[:, q * 2048:(q + 1) * 2048]
+
+    Y.dma_start(T.snd[:, 0:128], blk((r + 1) % n)).then_inc(S.ld1, 16)
+    A.dma_start(T.snd[:, 128:256], blk((r + 2) % n)).then_inc(S.ld2, 16)
+    Y.dma_start(T.snd[:, 256:384], blk((r + 3) % n)).then_inc(S.ld3, 16)
+    A.dma_start(T.tokc[:], T.tok[:]).then_inc(S.ldtok, 16)
+    Y.dma_start(T.part[:], T.par[:]).then_inc(S.ldpar, 16)
+    A.dma_start(T.own[:], blk(r)).then_inc(S.ldown, 16)
+    ne = [len(topo.engines(core, cores[(r + k) % n])) for k in (1, 2, 3)]
+    Y.wait_ge(S.sent, sum(ne))
+    Y.dma_start(T.kva[:, 16:2064], T.kv[:, mine * 2048:(mine + 1) * 2048]).then_inc(S.ldkv, 16)
+    Y.dma_start(T.kvb[:, 16:2064], T.kv[:, other * 2048:(other + 1) * 2048]).then_inc(S.ldkv, 16)
+
+    g.iota(T.pid[:], [[1, 1]], 0, 1).then_inc(S.gpid, 1)
+    g.iota(T.mb[:], [[-16, 8], [0, 16]], 0, 1, allow_small_or_imprecise_dtypes=True).then_inc(S.gmb, 1)
+    g.iota(T.ed[:], [[1, 128]], 0, -1).then_inc(S.ged, 1)
+    for k in (1, 2, 3):
+        dst = cores[(r + k) % n]
+        rid, pid = topo.addr(dst, core)
+        g.wait_ge(S["ld%d" % k], 16)
+        g.remote_dma(T["land%d" % k][:], T.snd[:, (k - 1) * 128:k * 128], S["arr%d" % k], S.sent, pid, rid, topo.mask(core, dst))
+    g.iota(T.mmod[:], [[0, 8], [1, 16]], 0, 0, allow_small_or_imprecise_dtypes=True).then_inc(S.gpre, 1)
+    g.iota(T.c16r[:], [[16, 128]], 0, 0, allow_small_or_imprecise_dtypes=True).then_inc(S.gpre, 1)
+    g.iota(T.ri[:], [[16, 4]], 1, 0).then_inc(S.gri, 1)
+    g.iota(T.yri[:], [[1, 64]], 1 - 1920, 0, allow_small_or_imprecise_dtypes=True).then_inc(S.gyr, 1)
+    g.iota(T.rst[:], [[0, 4], [30000, 16]], 0, 0, allow_small_or_imprecise_dtypes=True).then_inc(S.grst, 1)
+    g.iota(T.jrow[:], [[1, 1984]], 65, 0, allow_small_or_imprecise_dtypes=True).then_inc(S.gj, 1)
+
+    V.memset(T.zero[:], 0.0).then_inc(S.vz, 1)
+    V.memset(T.cst[:], 0.0078125).then_inc(S.vcst, 1)
+    V.wait_ge(S.gmb, 1)
+    for a in range(16):
+        V.tensor_scalar(T.sel[:, 128 * a:128 * a + 128], T.mb[:], float(a), None, Op.is_equal).then_inc(S.vsel, 1)
+    V.wait_ge(S.gpid, 1)
+    V.tensor_scalar(T.pmi[:], T.pid[:], 15, None, Op.bitwise_and).then_inc(S.vpmi, 1)
+    V.wait_ge(S.ged, 1)
+    V.tensor_scalar(T.d15[:], T.ed[:, 0:64], 15, None, Op.bitwise_and).then_inc(S.vd15, 1)
+    V.wait_ge(S.vpmi, 1)
+    V.tensor_copy(T.pmod[:], T.pmi[:]).then_inc(S.vpmod, 1)
+    V.wait_ge(S.ldtok, 16)
+    V.tensor_scalar(T.tokf[:], T.tokc[:], -2048.0, None, Op.add).then_inc(S.vtok, 1)
+    V.wait_ge(S.ldpar, 16)
+    V.tensor_scalar(T.parhi[:], T.part[:], 7, None, Op.arith_shift_right).then_inc(S.vpar, 1)
+    V.tensor_scalar(T.parlo[:], T.part[:], 127, None, Op.bitwise_and).then_inc(S.vpar, 1)
+    V.tensor_scalar(T.pcol[:], T.part[:], float(NODE + 1), None, Op.add).then_inc(S.vpar, 1)
+    V.wait_ge(S.vd15, 1)
+    V.tensor_scalar(T.c16[:], T.d15[:, 0:16], 8192.0, 2048.0, Op.mult, Op.max).then_inc(S.vc16, 1)
+    V.tensor_scalar(T.neg[:], T.d15[:], -2048.0, -2048.0, Op.mult, Op.max).then_inc(S.vc16, 1)
+    V.wait_ge(S.vpar, 3)
+    V.tensor_copy(T.hi[:], T.parhi[:]).then_inc(S.vlists, 1)
+    V.tensor_copy(T.lo[:], T.parlo[:]).then_inc(S.vlists, 1)
+    V.wait_ge(S.vpmod, 1)
+    V.tensor_scalar(T.mbt[:], T.ed[:], T.pmod[:], None, Op.add).then_inc(S.vmbt, 1)
+    V.wait_ge(S.vmbt, 1)
+    for i in range(16):
+        V.tensor_scalar(T.tab[:, 128 * i:128 * i + 128], T.mbt[:], float(i), 4096.0, Op.is_equal, Op.mult).then_inc(S.vtab, 1)
+    V.wait_ge(S.vc16, 2)
+    V.wait_ge(S.vlists, 2)
+    for b in range(4):
+        c0, c1 = max(C0, 32 * b), 32 * b + 32
+        V.wait_ge(S["ev%d" % b], 1)
+        V.tensor_tensor(T.tokx[:, 16 * c0:16 * c1], T.c16[:, 0:16].indirect(T.hi[:, c0:c1]), T.tokrow[:, 16 * c0:16 * c1],
+                        Op.add).then_inc(S.vtx, 1)
+    V.wait_ge(S.gyr, 1)
+    V.tensor_copy(T.yr[:], T.yri[:]).then_inc(S.vyr, 1)
+    V.wait_ge(S.gri, 1)
+    V.tensor_scalar(T.ls[:, 56:60], T.ri[:], T.pmod[:], None, Op.add).then_inc(S.vl, 1)
+    V.memset(T.kva[:, 0:16], 0.0).then_inc(S.vkz, 1)
+    V.memset(T.kvb[:, 0:16], 0.0).then_inc(S.vkz, 1)
+
+    P.wait_ge(S.vsel, 16)
+    P.wait_ge(S.vtok, 1)
+    for a in range(16):
+        P.matmul(T["tr%d" % (a // 4)][:, 128 * (a % 4):128 * (a % 4) + 128], T.sel[:, 128 * a:128 * a + 128], T.tokf[:],
+                 True, True).then_inc(S["ptr%d" % (a // 4)], 1)
+    P.wait_ge(S.vcst, 1)
+    P.wait_ge(S.gpre, 2)
+    for ps, c0, c1, sem in ((T.psa, C0, C1, S.poka), (T.psb, C1, C2, S.pokb)):
+        P.matmul(ps[:, 0:c1 - c0], T.mmod[:], T.cst[:, 0:c1 - c0], True, False).then_inc(sem, 1)
+        P.matmul(ps[:, 0:c1 - c0], T.cst[:], T.c16r[:, c0:c1], False, False).then_inc(sem, 1)
+    P.wait_ge(S.vtab, 16)
+    P.wait_ge(S.vyr, 1)
+    for h in range(2):
+        P.matmul(T.psf[:, 0:32], T.tab[:, 1024 * h:1024 * h + 128], T.yr[:, h:64:2], h == 0, False).then_inc(S.pf, 1)
+
+    def zeros(w, sem):
+        for k in range(4):
+            A.activation(w[:, NODE + 516 * k:NODE + 516 * k + 516], T.zero[:], Fn.Silu).then_inc(sem, 1)
+
+    A.wait_ge(S.vz, 1)
+    zeros(T.wa, S.afa)
+    for b in range(4):
+        A.wait_ge(S["ptr%d" % b], 4)
+        A.activation(T.tokrow[:, 512 * b:512 * b + 512], T["tr%d" % b][:], Fn.Identity).then_inc(S["ev%d" % b], 1)
+    zeros(T.wb, S.afb)
+
+    V.wait_ge(S.ldown, 16)
+    prev = T.own[:]
+    for k in (1, 2, 3):
+        V.wait_ge(S["arr%d" % k], ne[k - 1])
+        m = T.mx[:, 128 * k - 128:128 * k]
+        V.tensor_tensor(m, prev, T["land%d" % k][:], Op.max).then_inc(S["vm%d" % k], 1)
+        V.wait_ge(S["vm%d" % k], 1)
+        prev = m
+    V.tensor_scalar(T.tgt[:], prev, 4095, None, Op.bitwise_and).then_inc(S.vtgt, 1)
+    V.wait_ge(S.vtgt, 1)
+    V.wait_ge(S.vtx, 4)
+    for c0, c1, sem in ((C0, C1, S.veqa), (C1, C2, S.veqb)):
+        V.tensor_tensor(T.eq[:, 16 * c0:16 * c1], T.tgt[:, 0:128].indirect(T.lo[:, c0:c1]), T.tokx[:, 16 * c0:16 * c1],
+                        Op.is_equal).then_inc(sem, 1)
+    for ps, c0, c1, sin, sem in ((T.psa, C0, C1, S.veqa, S.poka), (T.psb, C1, C2, S.veqb, S.pokb)):
+        P.wait_ge(sin, 1)
+        for i in range(16):
+            P.matmul(ps[:, 0:c1 - c0], T.tab[:, 128 * i:128 * i + 128], T.eq[:, 16 * c0 + i:16 * c1:16],
+                     False, i == 15).then_inc(sem, 1)
+    for ps, c0, c1, sin, so, sem in ((T.psa, C0, C1, S.poka, S.voa, S.voffa), (T.psb, C1, C2, S.pokb, S.vob, S.voffb)):
+        V.wait_ge(sin, 18)
+        V.tensor_tensor(T.offi[:, c0:c1], ps[:, 0:c1 - c0], T.pcol[:, c0:c1], Op.min).then_inc(so, 1)
+        V.wait_ge(so, 1)
+        V.tensor_copy(T.off[:, c0:c1], T.offi[:, c0:c1]).then_inc(sem, 1)
+    A.wait_ge(S.afa, 4)
+    A.wait_ge(S.gj, 1)
+    A.wait_ge(S.voffa, 1)
+    A.activation(T.wa[:, 0:WIN].indirect(T.off[:, C0:C1]), T.jrow[:, 0:16 * NA], Fn.Silu).then_inc(S.asca, 1)
+    V.wait_ge(S.afb, 4)
+    V.wait_ge(S.gj, 1)
+    V.wait_ge(S.voffb, 1)
+    V.tensor_copy(T.wb[:, 0:WIN].indirect(T.off[:, C1:C2]), T.jrow[:, 16 * NA:1984]).then_inc(S.vscb, 1)
+    V.wait_ge(S.vl, 1)
+    V.wait_ge(S.vscb, 1)
+    V.wait_ge(S.grst, 1)
+    V.wait_ge(S.asca, 1)
+    lst = T.ls[:, 56:60]
+    for d in range(7):
+        e0, e1 = 64 * d, 64 * d + 64
+        V.tensor_tensor(T.xs[:, e0:e1], T.wa[:, NODE:WIN].indirect(lst), T.neg[:], Op.add).then_inc(S["x%d" % d], 1)
+        V.wait_ge(S["x%d" % d], 1)
+        V.tensor_tensor(T.ys[:, e0:e1], T.wb[:, NODE:WIN].indirect(lst), T.xs[:, e0:e1], Op.add).then_inc(S["y%d" % d], 1)
+        if d < 6:
+            V.wait_ge(S["y%d" % d], 1)
+            V.tensor_tensor_scan(T.ts[:, e0:e1], T.rst[:], T.ys[:, e0:e1], 0.0, Op.min, Op.max).then_inc(S["t%d" % d], 1)
+            V.wait_ge(S["t%d" % d], 1)
+            lst = T.ls[:, 8 * d:8 * d + 4]
+            V.tensor_copy(lst, T.ts[:, e0 + 15:e1:16]).then_inc(S["l%d" % d], 1)
+            V.wait_ge(S["l%d" % d], 1)
+        P.wait_ge(S["y%d" % d], 1)
+        for h in range(2):
+            i = 8 * h + d + 1
+            P.matmul(T.psf[:, 0:32], T.tab[:, 128 * i:128 * i + 128], T.ys[:, e0 + h:e1:2], False,
+                     d == 6 and h == 1).then_inc(S.pf, 1)
+    V.wait_ge(S.pf, 16)
+    V.tensor_scalar(T.fl[:], T.psf[:, 0:32], 1.0 / 65536, 1920 + 15.25, Op.mult, Op.add).then_inc(S.vfl, 1)
+    dst = cores[mate]
+    rid, pid = topo.addr(dst, core)
+    nl = len(topo.engines(core, dst))
+    g.wait_ge(S.vfl, 1)
+    g.remote_dma(T.fl2[:], T.fl[:], S.lst, S.lsent, pid, rid, topo.mask(core, dst))
+    g.wait_ge(S.lsent, nl)
+    V.wait_ge(S.vfl, 1)
+    V.wait_ge(S.ldkv, 32)
+    V.wait_ge(S.vkz, 2)
+    V.tensor_copy(T.ya[:], T.kva[:, 0:2064].indirect(T.fl[:])).then_inc(S.vya, 1)
+    Y.wait_ge(S.vya, 1)
+    Y.dma_start(T.y[:, 512 * mine:512 * mine + 512], T.ya[:]).then_inc(S.st1, 16)
+    V.wait_ge(S.lst, nl)
+    V.tensor_copy(T.yb[:], T.kvb[:, 0:2064].indirect(T.fl2[:, 0:16])).then_inc(S.vyb, 1)
+    A.wait_ge(S.ldkv, 32)
+    A.wait_ge(S.vkz, 2)
+    A.wait_ge(S.lst, nl)
+    A.activation(T.yc[:], T.kvb[:, 0:2064].indirect(T.fl2[:, 16:32]), Fn.Copy).then_inc(S.ayc, 1)
+    Y.wait_ge(S.vyb, 1)
+    Y.dma_start(T.y[:, 512 * other:512 * other + 256], T.yb[:]).then_inc(S.st1, 16)
+    A.wait_ge(S.ayc, 1)
+    A.dma_start(T.y[:, 512 * other + 256:512 * other + 512], T.yc[:]).then_inc(S.st2, 16)
+    Y.wait_ge(S.st1, 32)
+    A.wait_ge(S.st2, 16)

@@ -1,79 +1,37 @@
 from concourse.mybir import AluOpType as Op, ActivationFunctionType as Fn
 
-NA = 72
-C0, C1, C2 = 4, 4 + NA, 128
-NODE = 2048
-WIN = NODE + 2064
+CH = [(4, 28), (28, 80), (80, 128)]
+NODE, REG = 2048, 2064
+MID = NODE + REG
+
+I32 = ("sbuf", [128, 128], "int32")
+U16 = ("sbuf", [128, 128], "uint16")
+B16 = ("sbuf", [128, 128], "bfloat16")
+PS = ("psum", [128, 512], "float32")
+
+
+def sb(k, d="float32"):
+    return ("sbuf", [128, k], d)
+
 
 SCRATCH = {
-    "own": ("sbuf", [128, 128], "int32"),
-    "snd": ("sbuf", [128, 384], "int32"),
-    "land1": ("sbuf", [128, 128], "int32"),
-    "land2": ("sbuf", [128, 128], "int32"),
-    "land3": ("sbuf", [128, 128], "int32"),
-    "mx": ("sbuf", [128, 384], "int32"),
-    "tgt": ("sbuf", [128, 128], "int32"),
-    "tokc": ("sbuf", [128, 128], "int32"),
-    "tokf": ("sbuf", [128, 128], "float16"),
-    "part": ("sbuf", [128, 128], "int32"),
-    "parlo": ("sbuf", [128, 128], "int32"),
-    "parhi": ("sbuf", [128, 128], "int32"),
-    "lo": ("sbuf", [128, 128], "uint16"),
-    "hi": ("sbuf", [128, 128], "uint16"),
-    "pcol": ("sbuf", [128, 128], "float32"),
-    "pid": ("sbuf", [128, 1], "int32"),
-    "pmi": ("sbuf", [128, 1], "int32"),
-    "pmod": ("sbuf", [128, 1], "float32"),
-    "mb": ("sbuf", [128, 128], "bfloat16"),
-    "ed": ("sbuf", [128, 128], "int32"),
-    "mbt": ("sbuf", [128, 128], "bfloat16"),
-    "d15": ("sbuf", [128, 64], "int32"),
-    "c16": ("sbuf", [128, 16], "float32"),
-    "neg": ("sbuf", [128, 64], "float32"),
-    "sel": ("sbuf", [128, 2048], "float16"),
-    "tab": ("sbuf", [128, 2048], "float16"),
-    "cst": ("sbuf", [128, 128], "bfloat16"),
-    "mmod": ("sbuf", [128, 128], "bfloat16"),
-    "c16r": ("sbuf", [128, 128], "bfloat16"),
-    "rst": ("sbuf", [128, 64], "float32"),
-    "yri": ("sbuf", [128, 64], "float32"),
-    "yr": ("sbuf", [128, 64], "float16"),
-    "ri": ("sbuf", [128, 4], "int32"),
-    "jrow": ("sbuf", [128, 1984], "float32"),
-    "tokrow": ("sbuf", [128, 2048], "float32"),
-    "tokx": ("sbuf", [128, 2048], "float32"),
-    "eq": ("sbuf", [128, 2048], "float16"),
-    "offi": ("sbuf", [128, 128], "float32"),
-    "off": ("sbuf", [128, 128], "uint16"),
-    "zero": ("sbuf", [128, 516], "float32"),
-    "wa": ("sbuf", [128, WIN], "float32"),
-    "wb": ("sbuf", [128, WIN], "float32"),
-    "xs": ("sbuf", [128, 448], "float32"),
-    "ys": ("sbuf", [128, 448], "float16"),
-    "ts": ("sbuf", [128, 448], "float32"),
-    "ls": ("sbuf", [128, 64], "uint16"),
-    "fl": ("sbuf", [128, 32], "uint16"),
-    "fl2": ("sbuf", [128, 32], "uint16"),
-    "kva": ("sbuf", [128, 2064], "bfloat16"),
-    "kvb": ("sbuf", [128, 2064], "bfloat16"),
-    "ya": ("sbuf", [128, 512], "bfloat16"),
-    "yb": ("sbuf", [128, 256], "bfloat16"),
-    "yc": ("sbuf", [128, 256], "bfloat16"),
-    "tr0": ("psum", [128, 512], "float32"),
-    "tr1": ("psum", [128, 512], "float32"),
-    "tr2": ("psum", [128, 512], "float32"),
-    "tr3": ("psum", [128, 512], "float32"),
-    "psa": ("psum", [128, 512], "float32"),
-    "psb": ("psum", [128, 512], "float32"),
-    "psf": ("psum", [128, 512], "float32"),
+    "own": I32, "snd": sb(384, "int32"), "land1": I32, "land2": I32, "land3": I32, "mx": I32, "tgt": I32,
+    "tokc": I32, "tokf": sb(128, "float16"), "part": I32, "parlo": I32, "parhi": I32, "lo": U16, "hi": U16, "pcol": sb(128),
+    "pid": sb(1, "int32"), "pmi": sb(1, "int32"), "pmod": sb(1), "mb": B16, "ed": I32, "mbt": B16, "d15": I32,
+    "c16": sb(16), "msk": sb(128), "sel": sb(2048, "float16"), "tab": sb(2048, "float16"), "cst": B16, "kst": B16, "mmod": B16,
+    "c16r": B16, "rst": sb(128), "ri": sb(8, "int32"), "rk": sb(4, "int32"), "jrow": sb(1984), "tokrow": sb(2048),
+    "tokx": sb(2048), "eq": sb(2048, "float16"), "offi": sb(128), "off": U16, "zero": sb(516), "ww": sb(2 * MID),
+    "vs": sb(896, "float16"), "ts": sb(896), "ls": sb(64, "uint16"), "kl": sb(32, "uint16"), "k2": sb(32, "uint16"),
+    "kva": sb(2080, "bfloat16"), "kvb": sb(2080, "bfloat16"), "ya": sb(512, "bfloat16"), "yb": sb(512, "bfloat16"),
+    "tr0": PS, "tr1": PS, "tr2": PS, "tr3": PS, "ps0": PS, "ps1": PS, "ps2": PS,
 }
-SEMAPHORES = (["ld1", "ld2", "ld3", "ldown", "ldtok", "ldpar", "ldkv", "sent", "arr1", "arr2", "arr3", "lst", "lsent", "st1", "st2",
-               "gpid", "gmb", "ged", "gpre", "grst", "gyr", "gri", "gj",
-               "vz", "vkz", "vcst", "vsel", "vtok", "vpar", "vlists", "vpmi", "vpmod", "vmbt", "vtab", "vd15", "vc16", "vyr", "vl",
-               "vtx", "vm1", "vm2", "vm3", "vtgt", "veqa", "veqb", "voa", "vob", "voffa", "voffb", "vscb", "vfl", "vya", "vyb",
-               "afa", "afb", "ev0", "ev1", "ev2", "ev3", "asca", "ayc", "ptr0", "ptr1", "ptr2", "ptr3", "poka", "pokb", "pf"]
-              + ["x%d" % d for d in range(7)] + ["y%d" % d for d in range(7)] + ["t%d" % d for d in range(6)]
-              + ["l%d" % d for d in range(6)])
+SEMAPHORES = (["ld1", "ld2", "ld3", "ldown", "ldtok", "ldpar", "ldkv", "sent", "arr1", "arr2", "arr3", "lst", "lst2", "lsent",
+               "st1", "gpid", "gmb", "ged", "gpre", "grst", "gri",
+               "vz", "vkz", "vcst", "vsel", "vtok", "vpar", "vlists", "vpmi", "vpmod", "vmbt", "vtab", "vd15", "vc16", "vl",
+               "vtx", "vm1", "vm2", "vm3", "vtgt", "vyb", "aya", "ayb",
+               "afa", "afb", "ev0", "ev1", "ev2", "ev3", "ptr0", "ptr1", "ptr2", "ptr3"]
+              + ["%s%d" % (w, d) for w in ("x", "t", "l", "k") for d in range(8)]
+              + ["%s%d" % (w, c) for w in ("veq", "pok", "vo", "voff", "gj", "sc") for c in range(len(CH))])
 
 
 def rank_program(g, core, T, topo):
@@ -86,6 +44,9 @@ def rank_program(g, core, T, topo):
     V, A, P, Y = g.vector, g.scalar, g.tensor, g.sync
     mate = (r + 2) % n
     mine, other = r // 2, 1 - r // 2
+    low = {"allow_small_or_imprecise_dtypes": True}
+    last = len(CH) - 1
+    cb = CH[last][0]
 
     def blk(q):
         return T.best[:, q * 2048:(q + 1) * 2048]
@@ -96,171 +57,199 @@ def rank_program(g, core, T, topo):
     A.dma_start(T.tokc[:], T.tok[:]).then_inc(S.ldtok, 16)
     Y.dma_start(T.part[:], T.par[:]).then_inc(S.ldpar, 16)
     A.dma_start(T.own[:], blk(r)).then_inc(S.ldown, 16)
-    ne = [len(topo.engines(core, cores[(r + k) % n])) for k in (1, 2, 3)]
-    Y.wait_ge(S.sent, sum(ne))
-    Y.dma_start(T.kva[:, 16:2064], T.kv[:, mine * 2048:(mine + 1) * 2048]).then_inc(S.ldkv, 16)
-    Y.dma_start(T.kvb[:, 16:2064], T.kv[:, other * 2048:(other + 1) * 2048]).then_inc(S.ldkv, 16)
+    ne = {k: len(topo.engines(core, cores[(r + k) % n])) for k in (1, 2, 3)}
+    Y.wait_ge(S.vkz, 2)
+    Y.wait_ge(S.sent, sum(ne.values()))
+    Y.dma_start(T.kva[:, 17:2065], T.kv[:, mine * 2048:(mine + 1) * 2048]).then_inc(S.ldkv, 16)
+    Y.dma_start(T.kvb[:, 17:2065], T.kv[:, other * 2048:(other + 1) * 2048]).then_inc(S.ldkv, 16)
 
+    g.iota(T.mb[:], [[-16, 8], [0, 16]], 0, 1, **low).then_inc(S.gmb, 1)
     g.iota(T.pid[:], [[1, 1]], 0, 1).then_inc(S.gpid, 1)
-    g.iota(T.mb[:], [[-16, 8], [0, 16]], 0, 1, allow_small_or_imprecise_dtypes=True).then_inc(S.gmb, 1)
     g.iota(T.ed[:], [[1, 128]], 0, -1).then_inc(S.ged, 1)
+    g.iota(T.ri[:], [[16, 4], [REG, 2]], 1, 0).then_inc(S.gri, 1)
+    g.iota(T.rk[:], [[16, 4]], 1, 0).then_inc(S.gri, 1)
     for k in (1, 2, 3):
         dst = cores[(r + k) % n]
         rid, pid = topo.addr(dst, core)
         g.wait_ge(S["ld%d" % k], 16)
         g.remote_dma(T["land%d" % k][:], T.snd[:, (k - 1) * 128:k * 128], S["arr%d" % k], S.sent, pid, rid, topo.mask(core, dst))
-    g.iota(T.mmod[:], [[0, 8], [1, 16]], 0, 0, allow_small_or_imprecise_dtypes=True).then_inc(S.gpre, 1)
-    g.iota(T.c16r[:], [[16, 128]], 0, 0, allow_small_or_imprecise_dtypes=True).then_inc(S.gpre, 1)
-    g.iota(T.ri[:], [[16, 4]], 1, 0).then_inc(S.gri, 1)
-    g.iota(T.yri[:], [[1, 64]], 1 - 1920, 0, allow_small_or_imprecise_dtypes=True).then_inc(S.gyr, 1)
-    g.iota(T.rst[:], [[0, 4], [30000, 16]], 0, 0, allow_small_or_imprecise_dtypes=True).then_inc(S.grst, 1)
-    g.iota(T.jrow[:], [[1, 1984]], 65, 0, allow_small_or_imprecise_dtypes=True).then_inc(S.gj, 1)
+    g.iota(T.mmod[:], [[0, 8], [1, 16]], 0, 0, **low).then_inc(S.gpre, 1)
+    g.iota(T.c16r[:], [[16, 128]], 0, 0, **low).then_inc(S.gpre, 1)
+    for c, (c0, c1) in enumerate(CH):
+        g.iota(T.jrow[:, 16 * c0 - 64:16 * c1 - 64], [[1, 16 * (c1 - c0)]], 16 * c0 + 1, 0, **low).then_inc(S["gj%d" % c], 1)
+    g.iota(T.rst[:], [[0, 4], [3000, 32]], 0, 0, **low).then_inc(S.grst, 1)
 
     V.memset(T.zero[:], 0.0).then_inc(S.vz, 1)
-    V.memset(T.cst[:], 0.0078125).then_inc(S.vcst, 1)
     V.wait_ge(S.gmb, 1)
     for a in range(16):
         V.tensor_scalar(T.sel[:, 128 * a:128 * a + 128], T.mb[:], float(a), None, Op.is_equal).then_inc(S.vsel, 1)
     V.wait_ge(S.gpid, 1)
     V.tensor_scalar(T.pmi[:], T.pid[:], 15, None, Op.bitwise_and).then_inc(S.vpmi, 1)
     V.wait_ge(S.ged, 1)
-    V.tensor_scalar(T.d15[:], T.ed[:, 0:64], 15, None, Op.bitwise_and).then_inc(S.vd15, 1)
+    V.tensor_scalar(T.d15[:], T.ed[:], 15, None, Op.bitwise_and).then_inc(S.vd15, 1)
     V.wait_ge(S.vpmi, 1)
     V.tensor_copy(T.pmod[:], T.pmi[:]).then_inc(S.vpmod, 1)
+    V.wait_ge(S.vd15, 1)
+    V.tensor_scalar(T.c16[:], T.d15[:, 0:16], 8192.0, 2048.0, Op.mult, Op.max).then_inc(S.vc16, 1)
+    V.tensor_scalar(T.msk[:], T.d15[:], 0.0, None, Op.is_equal).then_inc(S.vc16, 1)
     V.wait_ge(S.ldtok, 16)
     V.tensor_scalar(T.tokf[:], T.tokc[:], -2048.0, None, Op.add).then_inc(S.vtok, 1)
     V.wait_ge(S.ldpar, 16)
     V.tensor_scalar(T.parhi[:], T.part[:], 7, None, Op.arith_shift_right).then_inc(S.vpar, 1)
     V.tensor_scalar(T.parlo[:], T.part[:], 127, None, Op.bitwise_and).then_inc(S.vpar, 1)
-    V.tensor_scalar(T.pcol[:], T.part[:], float(NODE + 1), None, Op.add).then_inc(S.vpar, 1)
-    V.wait_ge(S.vd15, 1)
-    V.tensor_scalar(T.c16[:], T.d15[:, 0:16], 8192.0, 2048.0, Op.mult, Op.max).then_inc(S.vc16, 1)
-    V.tensor_scalar(T.neg[:], T.d15[:], -2048.0, -2048.0, Op.mult, Op.max).then_inc(S.vc16, 1)
-    V.wait_ge(S.vpar, 3)
-    V.tensor_copy(T.hi[:], T.parhi[:]).then_inc(S.vlists, 1)
-    V.tensor_copy(T.lo[:], T.parlo[:]).then_inc(S.vlists, 1)
+    V.tensor_scalar(T.pcol[:, 0:cb], T.part[:, 0:cb], float(NODE + 1), None, Op.add).then_inc(S.vpar, 1)
+    V.tensor_scalar(T.pcol[:, cb:128], T.part[:, cb:128], 1.0, None, Op.add).then_inc(S.vpar, 1)
     V.wait_ge(S.vpmod, 1)
     V.tensor_scalar(T.mbt[:], T.ed[:], T.pmod[:], None, Op.add).then_inc(S.vmbt, 1)
+    V.wait_ge(S.vpar, 4)
+    V.tensor_copy(T.hi[:], T.parhi[:]).then_inc(S.vlists, 1)
+    V.tensor_copy(T.lo[:], T.parlo[:]).then_inc(S.vlists, 1)
     V.wait_ge(S.vmbt, 1)
     for i in range(16):
         V.tensor_scalar(T.tab[:, 128 * i:128 * i + 128], T.mbt[:], float(i), 4096.0, Op.is_equal, Op.mult).then_inc(S.vtab, 1)
+    V.memset(T.cst[:], 0.0078125).then_inc(S.vcst, 1)
+    V.memset(T.kst[:], 2048.0 - 65536.0).then_inc(S.vcst, 1)
+    V.memset(T.kva[:, 16:32], 0.0).then_inc(S.vkz, 1)
+    V.memset(T.kvb[:, 16:32], 0.0).then_inc(S.vkz, 1)
+    V.wait_ge(S.gri, 2)
+    V.tensor_scalar(T.ls[:, 0:8], T.ri[:], T.pmod[:], None, Op.add).then_inc(S.vl, 1)
+    V.tensor_scalar(T.kl[:, 0:4], T.rk[:], T.pmod[:], None, Op.add).then_inc(S.k0, 1)
     V.wait_ge(S.vc16, 2)
     V.wait_ge(S.vlists, 2)
     for b in range(4):
-        c0, c1 = max(C0, 32 * b), 32 * b + 32
+        c0, c1 = max(4, 32 * b), 32 * b + 32
         V.wait_ge(S["ev%d" % b], 1)
         V.tensor_tensor(T.tokx[:, 16 * c0:16 * c1], T.c16[:, 0:16].indirect(T.hi[:, c0:c1]), T.tokrow[:, 16 * c0:16 * c1],
                         Op.add).then_inc(S.vtx, 1)
-    V.wait_ge(S.gyr, 1)
-    V.tensor_copy(T.yr[:], T.yri[:]).then_inc(S.vyr, 1)
-    V.wait_ge(S.gri, 1)
-    V.tensor_scalar(T.ls[:, 56:60], T.ri[:], T.pmod[:], None, Op.add).then_inc(S.vl, 1)
-    V.memset(T.kva[:, 0:16], 0.0).then_inc(S.vkz, 1)
-    V.memset(T.kvb[:, 0:16], 0.0).then_inc(S.vkz, 1)
 
     P.wait_ge(S.vsel, 16)
     P.wait_ge(S.vtok, 1)
     for a in range(16):
         P.matmul(T["tr%d" % (a // 4)][:, 128 * (a % 4):128 * (a % 4) + 128], T.sel[:, 128 * a:128 * a + 128], T.tokf[:],
                  True, True).then_inc(S["ptr%d" % (a // 4)], 1)
-    P.wait_ge(S.vcst, 1)
+    P.wait_ge(S.vtab, 16)
+    P.wait_ge(S.vcst, 2)
     P.wait_ge(S.gpre, 2)
-    for ps, c0, c1, sem in ((T.psa, C0, C1, S.poka), (T.psb, C1, C2, S.pokb)):
+    for c, (c0, c1) in enumerate(CH):
+        ps, sem = T["ps%d" % c], S["pok%d" % c]
         P.matmul(ps[:, 0:c1 - c0], T.mmod[:], T.cst[:, 0:c1 - c0], True, False).then_inc(sem, 1)
         P.matmul(ps[:, 0:c1 - c0], T.cst[:], T.c16r[:, c0:c1], False, False).then_inc(sem, 1)
-    P.wait_ge(S.vtab, 16)
-    P.wait_ge(S.vyr, 1)
-    for h in range(2):
-        P.matmul(T.psf[:, 0:32], T.tab[:, 1024 * h:1024 * h + 128], T.yr[:, h:64:2], h == 0, False).then_inc(S.pf, 1)
+        if c == last:
+            P.matmul(ps[:, 0:c1 - c0], T.cst[:], T.kst[:, 0:c1 - c0], False, False).then_inc(sem, 1)
 
-    def zeros(w, sem):
+    def zeros(b, sem):
         for k in range(4):
-            A.activation(w[:, NODE + 516 * k:NODE + 516 * k + 516], T.zero[:], Fn.Silu).then_inc(sem, 1)
+            A.activation(T.ww[:, b + 516 * k:b + 516 * k + 516], T.zero[:], Fn.Silu).then_inc(sem, 1)
 
     A.wait_ge(S.vz, 1)
-    zeros(T.wa, S.afa)
+    zeros(NODE, S.afa)
     for b in range(4):
         A.wait_ge(S["ptr%d" % b], 4)
         A.activation(T.tokrow[:, 512 * b:512 * b + 512], T["tr%d" % b][:], Fn.Identity).then_inc(S["ev%d" % b], 1)
-    zeros(T.wb, S.afb)
+    zeros(MID, S.afb)
 
     V.wait_ge(S.ldown, 16)
     prev = T.own[:]
-    for k in (1, 2, 3):
-        V.wait_ge(S["arr%d" % k], ne[k - 1])
-        m = T.mx[:, 128 * k - 128:128 * k]
+    for k, m in ((1, T.tr1[:, 0:128]), (2, T.tr0[:, 0:128]), (3, T.mx[:])):
+        V.wait_ge(S["arr%d" % k], ne[k])
         V.tensor_tensor(m, prev, T["land%d" % k][:], Op.max).then_inc(S["vm%d" % k], 1)
         V.wait_ge(S["vm%d" % k], 1)
         prev = m
     V.tensor_scalar(T.tgt[:], prev, 4095, None, Op.bitwise_and).then_inc(S.vtgt, 1)
     V.wait_ge(S.vtgt, 1)
     V.wait_ge(S.vtx, 4)
-    for c0, c1, sem in ((C0, C1, S.veqa), (C1, C2, S.veqb)):
+
+    def match(c):
+        c0, c1 = CH[c]
         V.tensor_tensor(T.eq[:, 16 * c0:16 * c1], T.tgt[:, 0:128].indirect(T.lo[:, c0:c1]), T.tokx[:, 16 * c0:16 * c1],
-                        Op.is_equal).then_inc(sem, 1)
-    for ps, c0, c1, sin, sem in ((T.psa, C0, C1, S.veqa, S.poka), (T.psb, C1, C2, S.veqb, S.pokb)):
-        P.wait_ge(sin, 1)
+                        Op.not_equal if c == last else Op.is_equal).then_inc(S["veq%d" % c], 1)
+        P.wait_ge(S["veq%d" % c], 1)
         for i in range(16):
-            P.matmul(ps[:, 0:c1 - c0], T.tab[:, 128 * i:128 * i + 128], T.eq[:, 16 * c0 + i:16 * c1:16],
-                     False, i == 15).then_inc(sem, 1)
-    for ps, c0, c1, sin, so, sem in ((T.psa, C0, C1, S.poka, S.voa, S.voffa), (T.psb, C1, C2, S.pokb, S.vob, S.voffb)):
-        V.wait_ge(sin, 18)
-        V.tensor_tensor(T.offi[:, c0:c1], ps[:, 0:c1 - c0], T.pcol[:, c0:c1], Op.min).then_inc(so, 1)
-        V.wait_ge(so, 1)
-        V.tensor_copy(T.off[:, c0:c1], T.offi[:, c0:c1]).then_inc(sem, 1)
+            P.matmul(T["ps%d" % c][:, 0:c1 - c0], T.tab[:, 128 * i:128 * i + 128], T.eq[:, 16 * c0 + i:16 * c1:16],
+                     False, i == 15).then_inc(S["pok%d" % c], 1)
+
+    def offsets(c):
+        c0, c1 = CH[c]
+        V.wait_ge(S["pok%d" % c], 19 if c == last else 18)
+        V.tensor_tensor(T.offi[:, c0:c1], T["ps%d" % c][:, 0:c1 - c0], T.pcol[:, c0:c1],
+                        Op.max if c == last else Op.min).then_inc(S["vo%d" % c], 1)
+        V.wait_ge(S["vo%d" % c], 1)
+        V.tensor_copy(T.off[:, c0:c1], T.offi[:, c0:c1]).then_inc(S["voff%d" % c], 1)
+
+    match(0)
+    for c in range(1, last + 1):
+        match(c)
+        offsets(c - 1)
+    offsets(last)
     A.wait_ge(S.afa, 4)
-    A.wait_ge(S.gj, 1)
-    A.wait_ge(S.voffa, 1)
-    A.activation(T.wa[:, 0:WIN].indirect(T.off[:, C0:C1]), T.jrow[:, 0:16 * NA], Fn.Silu).then_inc(S.asca, 1)
+    for c in range(last):
+        c0, c1 = CH[c]
+        A.wait_ge(S["gj%d" % c], 1)
+        A.wait_ge(S["voff%d" % c], 1)
+        if c:
+            A.wait_ge(S["sc%d" % (c - 1)], 1)
+        A.activation(T.ww[:, 0:MID].indirect(T.off[:, c0:c1]), T.jrow[:, 16 * c0 - 64:16 * c1 - 64], Fn.Silu).then_inc(
+            S["sc%d" % c], 1)
+    c0, c1 = CH[last]
     V.wait_ge(S.afb, 4)
-    V.wait_ge(S.gj, 1)
-    V.wait_ge(S.voffb, 1)
-    V.tensor_copy(T.wb[:, 0:WIN].indirect(T.off[:, C1:C2]), T.jrow[:, 16 * NA:1984]).then_inc(S.vscb, 1)
+    V.wait_ge(S["gj%d" % last], 1)
+    V.wait_ge(S["voff%d" % last], 1)
+    V.tensor_copy(T.ww[:, MID:2 * MID].indirect(T.off[:, c0:c1]), T.jrow[:, 16 * c0 - 64:16 * c1 - 64]).then_inc(
+        S["sc%d" % last], 1)
     V.wait_ge(S.vl, 1)
-    V.wait_ge(S.vscb, 1)
     V.wait_ge(S.grst, 1)
-    V.wait_ge(S.asca, 1)
-    lst = T.ls[:, 56:60]
+    V.wait_ge(S["sc%d" % (last - 1)], 1)
+    V.wait_ge(S["sc%d" % last], 1)
+
+    def keys_of(d):
+        e0 = 128 * (d - 1)
+        V.tensor_copy(T.kl[:, 4 * d:4 * d + 4], T.ts[:, e0 + 31:e0 + 128:32]).then_inc(S["k%d" % d], 1)
+
     for d in range(7):
-        e0, e1 = 64 * d, 64 * d + 64
-        V.tensor_tensor(T.xs[:, e0:e1], T.wa[:, NODE:WIN].indirect(lst), T.neg[:], Op.add).then_inc(S["x%d" % d], 1)
+        e0, e1, a = 128 * d, 128 * d + 128, 8 * d + 8
+        V.tensor_tensor(T.vs[:, e0:e1], T.ww[:, NODE:MID + REG].indirect(T.ls[:, a - 8:a]), T.msk[:], Op.mult).then_inc(
+            S["x%d" % d], 1)
+        if d:
+            keys_of(d)
         V.wait_ge(S["x%d" % d], 1)
-        V.tensor_tensor(T.ys[:, e0:e1], T.wb[:, NODE:WIN].indirect(lst), T.xs[:, e0:e1], Op.add).then_inc(S["y%d" % d], 1)
+        V.tensor_tensor_scan(T.ts[:, e0:e1], T.rst[:], T.vs[:, e0:e1], 0.0, Op.min, Op.add).then_inc(S["t%d" % d], 1)
+        V.wait_ge(S["t%d" % d], 1)
         if d < 6:
-            V.wait_ge(S["y%d" % d], 1)
-            V.tensor_tensor_scan(T.ts[:, e0:e1], T.rst[:], T.ys[:, e0:e1], 0.0, Op.min, Op.max).then_inc(S["t%d" % d], 1)
-            V.wait_ge(S["t%d" % d], 1)
-            lst = T.ls[:, 8 * d:8 * d + 4]
-            V.tensor_copy(lst, T.ts[:, e0 + 15:e1:16]).then_inc(S["l%d" % d], 1)
-            V.wait_ge(S["l%d" % d], 1)
-        P.wait_ge(S["y%d" % d], 1)
-        for h in range(2):
-            i = 8 * h + d + 1
-            P.matmul(T.psf[:, 0:32], T.tab[:, 128 * i:128 * i + 128], T.ys[:, e0 + h:e1:2], False,
-                     d == 6 and h == 1).then_inc(S.pf, 1)
-    V.wait_ge(S.pf, 16)
-    V.tensor_scalar(T.fl[:], T.psf[:, 0:32], 1.0 / 65536, 1920 + 15.25, Op.mult, Op.add).then_inc(S.vfl, 1)
+            V.tensor_copy(T.ls[:, a:a + 8:2], T.ts[:, e0 + 31:e1:32]).then_inc(S["l%d" % d], 1)
+            V.tensor_scalar(T.ls[:, a + 1:a + 8:2], T.ts[:, e0 + 31:e1:32], float(REG), None, Op.add).then_inc(S["l%d" % d], 1)
+            V.wait_ge(S["l%d" % d], 2)
+    keys_of(7)
     dst = cores[mate]
     rid, pid = topo.addr(dst, core)
     nl = len(topo.engines(core, dst))
-    g.wait_ge(S.vfl, 1)
-    g.remote_dma(T.fl2[:], T.fl[:], S.lst, S.lsent, pid, rid, topo.mask(core, dst))
-    g.wait_ge(S.lsent, nl)
-    V.wait_ge(S.vfl, 1)
-    V.wait_ge(S.ldkv, 32)
-    V.wait_ge(S.vkz, 2)
-    V.tensor_copy(T.ya[:], T.kva[:, 0:2064].indirect(T.fl[:])).then_inc(S.vya, 1)
-    Y.wait_ge(S.vya, 1)
-    Y.dma_start(T.y[:, 512 * mine:512 * mine + 512], T.ya[:]).then_inc(S.st1, 16)
-    V.wait_ge(S.lst, nl)
-    V.tensor_copy(T.yb[:], T.kvb[:, 0:2064].indirect(T.fl2[:, 0:16])).then_inc(S.vyb, 1)
+    for d in range(1, 6):
+        g.wait_ge(S["k%d" % d], 1)
+    g.remote_dma(T.k2[:, 4:24], T.kl[:, 4:24], S.lst, S.lsent, pid, rid, topo.mask(core, dst))
+    g.wait_ge(S.k6, 1)
+    g.wait_ge(S.k7, 1)
+    g.remote_dma(T.k2[:, 24:32], T.kl[:, 24:32], S.lst2, S.lsent, pid, rid, topo.mask(core, dst))
+    g.wait_ge(S.lsent, 2 * nl)
+    ka, kb = T.kva[:, 16:2065], T.kvb[:, 16:2065]
     A.wait_ge(S.ldkv, 32)
-    A.wait_ge(S.vkz, 2)
+    for d in range(8):
+        A.wait_ge(S["k%d" % d], 1)
+        A.activation(T.ya[:, d:512:8], ka.indirect(T.kl[:, 4 * d:4 * d + 4]), Fn.Copy).then_inc(S.aya, 1)
+    Y.wait_ge(S.aya, 8)
+    Y.dma_start(T.y[:, 512 * mine:512 * mine + 512], T.ya[:]).then_inc(S.st1, 16)
+    V.wait_ge(S.ldkv, 32)
+    V.wait_ge(S.k0, 1)
+    V.tensor_copy(T.yb[:, 0:512:8], kb.indirect(T.kl[:, 0:4])).then_inc(S.vyb, 1)
+    V.wait_ge(S.lst, nl)
     A.wait_ge(S.lst, nl)
-    A.activation(T.yc[:], T.kvb[:, 0:2064].indirect(T.fl2[:, 16:32]), Fn.Copy).then_inc(S.ayc, 1)
-    Y.wait_ge(S.vyb, 1)
-    Y.dma_start(T.y[:, 512 * other:512 * other + 256], T.yb[:]).then_inc(S.st1, 16)
-    A.wait_ge(S.ayc, 1)
-    A.dma_start(T.y[:, 512 * other + 256:512 * other + 512], T.yc[:]).then_inc(S.st2, 16)
+    for d in (1, 2):
+        V.tensor_copy(T.yb[:, d:512:8], kb.indirect(T.k2[:, 4 * d:4 * d + 4])).then_inc(S.vyb, 1)
+    for d in (3, 4, 5):
+        A.activation(T.yb[:, d:512:8], kb.indirect(T.k2[:, 4 * d:4 * d + 4]), Fn.Copy).then_inc(S.ayb, 1)
+    V.wait_ge(S.lst2, nl)
+    A.wait_ge(S.lst2, nl)
+    V.tensor_copy(T.yb[:, 6:512:8], kb.indirect(T.k2[:, 24:28])).then_inc(S.vyb, 1)
+    A.activation(T.yb[:, 7:512:8], kb.indirect(T.k2[:, 28:32]), Fn.Copy).then_inc(S.ayb, 1)
+    Y.wait_ge(S.vyb, 4)
+    Y.wait_ge(S.ayb, 4)
+    Y.dma_start(T.y[:, 512 * other:512 * other + 512], T.yb[:]).then_inc(S.st1, 16)
     Y.wait_ge(S.st1, 32)
-    A.wait_ge(S.st2, 16)

@@ -18,8 +18,8 @@ SCRATCH = {
     "own": I32, "snd": sb(384, "int32"), "land1": I32, "land2": I32, "land3": I32, "mx": I32, "tgt": I32,
     "tokc": I32, "tokf": sb(128, "float16"), "part": I32, "parlo": I32, "parhi": I32, "lo": U16, "hi": U16, "pcol": sb(128),
     "pid": sb(1, "int32"), "pmi": sb(1, "int32"), "pmod": sb(1), "mb": B16, "ed": I32, "mbt": B16, "d15": I32,
-    "c16": sb(16), "msk": sb(128), "sel": sb(2048, "float16"), "tab": sb(2048, "float16"), "cst": B16, "kst": B16, "mmod": B16,
-    "c16r": B16, "rst": sb(128), "ri": sb(8, "int32"), "rk": sb(4, "int32"), "jrow": sb(1984), "tokrow": sb(2048),
+    "c16": sb(16), "msk": sb(64), "sel": sb(2048, "float16"), "tab": sb(2048, "float16"), "cst": B16, "kst": B16, "mmod": B16,
+    "c16r": B16, "rst": sb(64), "ri": sb(8, "int32"), "rk": sb(4, "int32"), "jrow": sb(1984), "tokrow": sb(2048),
     "tokx": sb(2048), "eq": sb(2048, "float16"), "offi": sb(128), "off": U16, "zero": sb(516), "ww": sb(2 * MID),
     "vs": sb(896, "float16"), "ts": sb(896), "ls": sb(64, "uint16"), "kl": sb(32, "uint16"), "k2": sb(32, "uint16"),
     "kva": sb(2080, "bfloat16"), "kvb": sb(2080, "bfloat16"), "ya": sb(512, "bfloat16"), "yb": sb(512, "bfloat16"),
@@ -28,9 +28,10 @@ SCRATCH = {
 SEMAPHORES = (["ld1", "ld2", "ld3", "ldown", "ldtok", "ldpar", "ldkv", "sent", "arr1", "arr2", "arr3", "lst", "lst2", "lsent",
                "st1", "gpid", "gmb", "ged", "gpre", "grst", "gri",
                "vz", "vkz", "vcst", "vsel", "vtok", "vpar", "vlists", "vpmi", "vpmod", "vmbt", "vtab", "vd15", "vc16", "vl",
-               "vtx", "vm1", "vm2", "vm3", "vtgt", "vyb", "aya", "ayb",
+               "vtx", "vm1", "vm2", "vm30", "vm31", "vtgt", "vyb", "aya", "ayb",
                "afa", "afb", "ev0", "ev1", "ev2", "ev3", "ptr0", "ptr1", "ptr2", "ptr3"]
-              + ["%s%d" % (w, d) for w in ("x", "t", "l", "k") for d in range(8)]
+              + ["%s%d%d" % (w, d, h) for w in ("x", "t", "l") for d in range(7) for h in range(2)]
+              + ["k%d" % d for d in range(8)]
               + ["%s%d" % (w, c) for w in ("veq", "pok", "vo", "voff", "gj", "sc") for c in range(len(CH))])
 
 
@@ -77,7 +78,7 @@ def rank_program(g, core, T, topo):
     g.iota(T.c16r[:], [[16, 128]], 0, 0, **low).then_inc(S.gpre, 1)
     for c, (c0, c1) in enumerate(CH):
         g.iota(T.jrow[:, 16 * c0 - 64:16 * c1 - 64], [[1, 16 * (c1 - c0)]], 16 * c0 + 1, 0, **low).then_inc(S["gj%d" % c], 1)
-    g.iota(T.rst[:], [[0, 4], [3000, 32]], 0, 0, **low).then_inc(S.grst, 1)
+    g.iota(T.rst[:], [[0, 2], [3000, 32]], 0, 0, **low).then_inc(S.grst, 1)
 
     V.memset(T.zero[:], 0.0).then_inc(S.vz, 1)
     V.wait_ge(S.gmb, 1)
@@ -91,7 +92,7 @@ def rank_program(g, core, T, topo):
     V.tensor_copy(T.pmod[:], T.pmi[:]).then_inc(S.vpmod, 1)
     V.wait_ge(S.vd15, 1)
     V.tensor_scalar(T.c16[:], T.d15[:, 0:16], 8192.0, 2048.0, Op.mult, Op.max).then_inc(S.vc16, 1)
-    V.tensor_scalar(T.msk[:], T.d15[:], 0.0, None, Op.is_equal).then_inc(S.vc16, 1)
+    V.tensor_scalar(T.msk[:], T.d15[:, 0:64], 0.0, None, Op.is_equal).then_inc(S.vc16, 1)
     V.wait_ge(S.ldtok, 16)
     V.tensor_scalar(T.tokf[:], T.tokc[:], -2048.0, None, Op.add).then_inc(S.vtok, 1)
     V.wait_ge(S.ldpar, 16)
@@ -149,14 +150,20 @@ def rank_program(g, core, T, topo):
     zeros(MID, S.afb)
 
     V.wait_ge(S.ldown, 16)
-    prev = T.own[:]
-    for k, m in ((1, T.tr1[:, 0:128]), (2, T.tr0[:, 0:128]), (3, T.mx[:])):
+    prev = T.own
+    for k, m in ((1, T.tr1), (2, T.tr0)):
         V.wait_ge(S["arr%d" % k], ne[k])
-        V.tensor_tensor(m, prev, T["land%d" % k][:], Op.max).then_inc(S["vm%d" % k], 1)
+        V.tensor_tensor(m[:, 0:128], prev[:, 0:128], T["land%d" % k][:], Op.max).then_inc(S["vm%d" % k], 1)
         V.wait_ge(S["vm%d" % k], 1)
         prev = m
-    V.tensor_scalar(T.tgt[:], prev, 4095, None, Op.bitwise_and).then_inc(S.vtgt, 1)
-    V.wait_ge(S.vtgt, 1)
+    V.wait_ge(S.arr3, ne[3])
+    for h in range(2):
+        V.tensor_tensor(T.mx[:, 64 * h:64 * h + 64], prev[:, 64 * h:64 * h + 64], T.land3[:, 64 * h:64 * h + 64],
+                        Op.max).then_inc(S["vm3%d" % h], 1)
+    for h in range(2):
+        V.wait_ge(S["vm3%d" % h], 1)
+        V.tensor_scalar(T.tgt[:, 64 * h:64 * h + 64], T.mx[:, 64 * h:64 * h + 64], 4095, None, Op.bitwise_and).then_inc(S.vtgt, 1)
+    V.wait_ge(S.vtgt, 2)
     V.wait_ge(S.vtx, 4)
 
     def match(c):
@@ -206,18 +213,26 @@ def rank_program(g, core, T, topo):
         V.tensor_copy(T.kl[:, 4 * d:4 * d + 4], T.ts[:, e0 + 31:e0 + 128:32]).then_inc(S["k%d" % d], 1)
 
     for d in range(7):
-        e0, e1, a = 128 * d, 128 * d + 128, 8 * d + 8
-        V.tensor_tensor(T.vs[:, e0:e1], T.ww[:, NODE:MID + REG].indirect(T.ls[:, a - 8:a]), T.msk[:], Op.mult).then_inc(
-            S["x%d" % d], 1)
+        for h in range(2):
+            e0, b = 128 * d + 64 * h, 8 * d + 4 * h
+            if d:
+                V.wait_ge(S["l%d%d" % (d - 1, h)], 2)
+            V.tensor_tensor(T.vs[:, e0:e0 + 64], T.ww[:, NODE:MID + REG].indirect(T.ls[:, b:b + 4]), T.msk[:], Op.mult).then_inc(
+                S["x%d%d" % (d, h)], 1)
         if d:
             keys_of(d)
-        V.wait_ge(S["x%d" % d], 1)
-        V.tensor_tensor_scan(T.ts[:, e0:e1], T.rst[:], T.vs[:, e0:e1], 0.0, Op.min, Op.add).then_inc(S["t%d" % d], 1)
-        V.wait_ge(S["t%d" % d], 1)
-        if d < 6:
-            V.tensor_copy(T.ls[:, a:a + 8:2], T.ts[:, e0 + 31:e1:32]).then_inc(S["l%d" % d], 1)
-            V.tensor_scalar(T.ls[:, a + 1:a + 8:2], T.ts[:, e0 + 31:e1:32], float(REG), None, Op.add).then_inc(S["l%d" % d], 1)
-            V.wait_ge(S["l%d" % d], 2)
+        for h in range(2):
+            e0 = 128 * d + 64 * h
+            V.wait_ge(S["x%d%d" % (d, h)], 1)
+            V.tensor_tensor_scan(T.ts[:, e0:e0 + 64], T.rst[:], T.vs[:, e0:e0 + 64], 0.0, Op.min, Op.add).then_inc(
+                S["t%d%d" % (d, h)], 1)
+        for h in range(2):
+            e0, b = 128 * d + 64 * h, 8 * d + 8 + 4 * h
+            V.wait_ge(S["t%d%d" % (d, h)], 1)
+            if d < 6:
+                V.tensor_copy(T.ls[:, b:b + 4:2], T.ts[:, e0 + 31:e0 + 64:32]).then_inc(S["l%d%d" % (d, h)], 1)
+                V.tensor_scalar(T.ls[:, b + 1:b + 4:2], T.ts[:, e0 + 31:e0 + 64:32], float(REG), None, Op.add).then_inc(
+                    S["l%d%d" % (d, h)], 1)
     keys_of(7)
     dst = cores[mate]
     rid, pid = topo.addr(dst, core)

@@ -1,12 +1,18 @@
 from concourse.mybir import AluOpType as Op, ActivationFunctionType as Fn
 
-CH = [(4, 28), (28, 80), (80, 128)]
+CH = [(4, 46), (46, 96), (96, 128)]
+VS = 64
 NODE, REG = 2048, 2064
 MID = NODE + REG
+ZC = 258
+NZ = REG // ZC
+ZV = 2
+HV = 12
 
 I32 = ("sbuf", [128, 128], "int32")
 U16 = ("sbuf", [128, 128], "uint16")
 B16 = ("sbuf", [128, 128], "bfloat16")
+F16 = ("sbuf", [128, 128], "float16")
 PS = ("psum", [128, 512], "float32")
 
 
@@ -16,23 +22,23 @@ def sb(k, d="float32"):
 
 SCRATCH = {
     "own": I32, "snd": sb(384, "int32"), "land1": I32, "land2": I32, "land3": I32, "mx": I32, "tgt": I32,
-    "tokc": I32, "tokf": sb(128, "float16"), "part": I32, "parlo": I32, "parhi": I32, "lo": U16, "hi": U16, "pcol": sb(128),
-    "pid": sb(1, "int32"), "pmi": sb(1, "int32"), "pmod": sb(1), "mb": B16, "ed": I32, "mbt": B16, "d15": I32,
-    "c16": sb(16), "msk": sb(64), "sel": sb(2048, "float16"), "tab": sb(2048, "float16"), "cst": B16, "kst": B16, "mmod": B16,
-    "c16r": B16, "rst": sb(64), "ri": sb(8, "int32"), "rk": sb(4, "int32"), "jrow": sb(1984), "tokrow": sb(2048),
-    "tokx": sb(2048), "eq": sb(2048, "float16"), "offi": sb(128), "off": U16, "zero": sb(516), "ww": sb(2 * MID),
-    "vs": sb(896, "float16"), "ts": sb(896), "ls": sb(64, "uint16"), "kl": sb(32, "uint16"), "k2": sb(32, "uint16"),
+    "tokc": I32, "tokf": F16, "part": I32, "parlo": I32, "parhi": I32, "lo": U16, "hif": B16, "pcol": sb(128),
+    "sm": sb(32, "int32"), "d15": sb(32, "int32"), "pmod": sb(1), "pb": sb(1), "qc": sb(1), "mb": B16, "ab": B16, "grp": B16,
+    "mcol": sb(16, "bfloat16"), "msk": sb(32), "mr": B16, "mrf": F16, "hx": sb(2048, "bfloat16"),
+    "sel": sb(2048, "float16"), "wi": sb(144, "bfloat16"), "tab": sb(144, "float16"), "cst": B16,
+    "c16r": B16, "rst": sb(64), "rk": sb(4, "int32"), "jrow": sb(1984),
+    "tokx": sb(2048), "eq": sb(2048, "float16"), "offi": sb(128), "off": U16, "zero": sb(ZC), "ww": sb(2 * MID),
+    "vs": sb(896, "float16"), "ts": sb(896), "ls": sb(32, "uint16"), "k2": sb(32, "uint16"),
     "kva": sb(2080, "bfloat16"), "kvb": sb(2080, "bfloat16"), "ya": sb(512, "bfloat16"), "yb": sb(512, "bfloat16"),
-    "tr0": PS, "tr1": PS, "tr2": PS, "tr3": PS, "ps0": PS, "ps1": PS, "ps2": PS,
+    "tr0": PS, "tr1": PS, "tr2": PS, "tr3": PS, "ps0": PS, "ps1": PS, "ps2": PS, "pm": PS,
 }
 SEMAPHORES = (["ld1", "ld2", "ld3", "ldown", "ldtok", "ldpar", "ldkv", "sent", "arr1", "arr2", "arr3", "lst", "lst2", "lsent",
-               "st1", "gpid", "gmb", "ged", "gpre", "grst", "gri",
-               "vz", "vkz", "vcst", "vsel", "vtok", "vpar", "vlists", "vpmi", "vpmod", "vmbt", "vtab", "vd15", "vc16", "vl",
-               "vtx", "vm1", "vm2", "vm30", "vm31", "vtgt", "vyb", "aya", "ayb",
-               "afa", "afb", "ev0", "ev1", "ev2", "ev3", "ptr0", "ptr1", "ptr2", "ptr3"]
+               "st1", "gsm", "gmb", "gmr", "gwi", "gpre", "grst", "gri",
+               "vz", "vzb", "vkz", "vcst", "vsel", "vmr", "vtok", "vpar", "vhi", "vhf", "vhx", "ahx", "vlist", "vpmod", "vpb", "vqc",
+               "vtab", "vd15", "vmsk", "vmcol", "aab", "vgrp", "vm1", "vm2", "vm30", "vm31", "vtgt", "vyb", "aya", "ayb", "k0",
+               "afa", "afb", "ev0", "ev1", "ev2", "ev3", "ptr0", "ptr1", "ptr2", "ptr3", "sca0", "sca1", "scv0", "scv1"]
               + ["%s%d%d" % (w, d, h) for w in ("x", "t", "l") for d in range(7) for h in range(2)]
-              + ["k%d" % d for d in range(8)]
-              + ["%s%d" % (w, c) for w in ("veq", "pok", "vo", "voff", "gj", "sc") for c in range(len(CH))])
+              + ["%s%d" % (w, c) for w in ("veq", "pok", "vo", "voff", "gj") for c in range(len(CH))])
 
 
 def rank_program(g, core, T, topo):
@@ -46,17 +52,16 @@ def rank_program(g, core, T, topo):
     mate = (r + 2) % n
     mine, other = r // 2, 1 - r // 2
     low = {"allow_small_or_imprecise_dtypes": True}
-    last = len(CH) - 1
-    cb = CH[last][0]
+    ps = [T.ps0, T.ps1, T.ps2]
 
     def blk(q):
         return T.best[:, q * 2048:(q + 1) * 2048]
 
     Y.dma_start(T.snd[:, 0:128], blk((r + 1) % n)).then_inc(S.ld1, 16)
-    A.dma_start(T.snd[:, 128:256], blk((r + 2) % n)).then_inc(S.ld2, 16)
-    Y.dma_start(T.snd[:, 256:384], blk((r + 3) % n)).then_inc(S.ld3, 16)
     A.dma_start(T.tokc[:], T.tok[:]).then_inc(S.ldtok, 16)
     Y.dma_start(T.part[:], T.par[:]).then_inc(S.ldpar, 16)
+    A.dma_start(T.snd[:, 128:256], blk((r + 2) % n)).then_inc(S.ld2, 16)
+    Y.dma_start(T.snd[:, 256:384], blk((r + 3) % n)).then_inc(S.ld3, 16)
     A.dma_start(T.own[:], blk(r)).then_inc(S.ldown, 16)
     ne = {k: len(topo.engines(core, cores[(r + k) % n])) for k in (1, 2, 3)}
     Y.wait_ge(S.vkz, 2)
@@ -65,16 +70,15 @@ def rank_program(g, core, T, topo):
     Y.dma_start(T.kvb[:, 17:2065], T.kv[:, other * 2048:(other + 1) * 2048]).then_inc(S.ldkv, 16)
 
     g.iota(T.mb[:], [[-16, 8], [0, 16]], 0, 1, **low).then_inc(S.gmb, 1)
-    g.iota(T.pid[:], [[1, 1]], 0, 1).then_inc(S.gpid, 1)
-    g.iota(T.ed[:], [[1, 128]], 0, -1).then_inc(S.ged, 1)
-    g.iota(T.ri[:], [[16, 4], [REG, 2]], 1, 0).then_inc(S.gri, 1)
-    g.iota(T.rk[:], [[16, 4]], 1, 0).then_inc(S.gri, 1)
+    g.iota(T.sm[:], [[-1, 32]], 0, 1).then_inc(S.gsm, 1)
+    g.iota(T.mr[:], [[0, 8], [-4096, 16]], 0, 0, **low).then_inc(S.gmr, 1)
     for k in (1, 2, 3):
         dst = cores[(r + k) % n]
         rid, pid = topo.addr(dst, core)
         g.wait_ge(S["ld%d" % k], 16)
         g.remote_dma(T["land%d" % k][:], T.snd[:, (k - 1) * 128:k * 128], S["arr%d" % k], S.sent, pid, rid, topo.mask(core, dst))
-    g.iota(T.mmod[:], [[0, 8], [1, 16]], 0, 0, **low).then_inc(S.gpre, 1)
+    g.iota(T.rk[:], [[16, 4]], 1, 0).then_inc(S.gri, 1)
+    g.iota(T.wi[:], [[1, 144]], -15, -1, **low).then_inc(S.gwi, 1)
     g.iota(T.c16r[:], [[16, 128]], 0, 0, **low).then_inc(S.gpre, 1)
     for c, (c0, c1) in enumerate(CH):
         g.iota(T.jrow[:, 16 * c0 - 64:16 * c1 - 64], [[1, 16 * (c1 - c0)]], 16 * c0 + 1, 0, **low).then_inc(S["gj%d" % c], 1)
@@ -84,176 +88,213 @@ def rank_program(g, core, T, topo):
     V.wait_ge(S.gmb, 1)
     for a in range(16):
         V.tensor_scalar(T.sel[:, 128 * a:128 * a + 128], T.mb[:], float(a), None, Op.is_equal).then_inc(S.vsel, 1)
-    V.wait_ge(S.gpid, 1)
-    V.tensor_scalar(T.pmi[:], T.pid[:], 15, None, Op.bitwise_and).then_inc(S.vpmi, 1)
-    V.wait_ge(S.ged, 1)
-    V.tensor_scalar(T.d15[:], T.ed[:], 15, None, Op.bitwise_and).then_inc(S.vd15, 1)
-    V.wait_ge(S.vpmi, 1)
-    V.tensor_copy(T.pmod[:], T.pmi[:]).then_inc(S.vpmod, 1)
+    V.wait_ge(S.gsm, 1)
+    V.tensor_scalar(T.d15[:], T.sm[:], 15, None, Op.bitwise_and).then_inc(S.vd15, 1)
+    V.wait_ge(S.gmr, 1)
+    V.tensor_copy(T.mrf[:], T.mr[:]).then_inc(S.vmr, 1)
+    V.wait_ge(S.aab, 1)
+    V.tensor_scalar(T.grp[:], T.ab[:], 8.0, 2048.0, Op.is_lt, Op.mult).then_inc(S.vgrp, 1)
     V.wait_ge(S.vd15, 1)
-    V.tensor_scalar(T.c16[:], T.d15[:, 0:16], 8192.0, 2048.0, Op.mult, Op.max).then_inc(S.vc16, 1)
-    V.tensor_scalar(T.msk[:], T.d15[:, 0:64], 0.0, None, Op.is_equal).then_inc(S.vc16, 1)
+    V.tensor_scalar(T.msk[:], T.d15[:], 0.0, None, Op.is_equal).then_inc(S.vmsk, 1)
+    V.tensor_scalar(T.mcol[:], T.d15[:, 0:16], 0.0, None, Op.is_equal).then_inc(S.vmcol, 1)
+    V.tensor_copy(T.pmod[:], T.d15[:, 0:1]).then_inc(S.vpmod, 1)
+    V.memset(T.cst[:], 2.0 ** -19).then_inc(S.vcst, 1)
+    V.wait_ge(S.ldpar, 16)
+    V.tensor_scalar(T.parhi[:], T.part[:], 7, None, Op.arith_shift_right).then_inc(S.vhi, 1)
     V.wait_ge(S.ldtok, 16)
     V.tensor_scalar(T.tokf[:], T.tokc[:], -2048.0, None, Op.add).then_inc(S.vtok, 1)
-    V.wait_ge(S.ldpar, 16)
-    V.tensor_scalar(T.parhi[:], T.part[:], 7, None, Op.arith_shift_right).then_inc(S.vpar, 1)
-    V.tensor_scalar(T.parlo[:], T.part[:], 127, None, Op.bitwise_and).then_inc(S.vpar, 1)
-    V.tensor_scalar(T.pcol[:, 0:cb], T.part[:, 0:cb], float(NODE + 1), None, Op.add).then_inc(S.vpar, 1)
-    V.tensor_scalar(T.pcol[:, cb:128], T.part[:, cb:128], 1.0, None, Op.add).then_inc(S.vpar, 1)
+    V.wait_ge(S.vhi, 1)
+    V.tensor_scalar(T.hif[:], T.parhi[:], 2.0, None, Op.mult).then_inc(S.vhf, 1)
     V.wait_ge(S.vpmod, 1)
-    V.tensor_scalar(T.mbt[:], T.ed[:], T.pmod[:], None, Op.add).then_inc(S.vmbt, 1)
-    V.wait_ge(S.vpar, 4)
-    V.tensor_copy(T.hi[:], T.parhi[:]).then_inc(S.vlists, 1)
-    V.tensor_copy(T.lo[:], T.parlo[:]).then_inc(S.vlists, 1)
-    V.wait_ge(S.vmbt, 1)
-    for i in range(16):
-        V.tensor_scalar(T.tab[:, 128 * i:128 * i + 128], T.mbt[:], float(i), 4096.0, Op.is_equal, Op.mult).then_inc(S.vtab, 1)
-    V.memset(T.cst[:], 0.0078125).then_inc(S.vcst, 1)
-    V.memset(T.kst[:], 2048.0 - 65536.0).then_inc(S.vcst, 1)
+    V.tensor_scalar(T.pb[:], T.pmod[:], -4096.0, 2048.0, Op.mult, Op.add).then_inc(S.vpb, 1)
+    V.wait_ge(S.vmcol, 1)
+    V.wait_ge(S.vhf, 1)
+    for i in range(HV):
+        V.tensor_scalar(T.hx[:, i:2048:16], T.hif[:], T.mcol[:, i:i + 1], None, Op.mult).then_inc(S.vhx, 1)
+    V.tensor_scalar(T.parlo[:], T.part[:], 127, None, Op.bitwise_and).then_inc(S.vpar, 1)
+    V.tensor_scalar(T.qc[:], T.pmod[:], -1.0 / 4096, (NODE + 1) / 4096, Op.mult, Op.add).then_inc(S.vqc, 1)
+    V.wait_ge(S.vpar, 1)
+    V.tensor_copy(T.lo[:], T.parlo[:]).then_inc(S.vlist, 1)
+    V.wait_ge(S.vqc, 1)
+    V.tensor_scalar(T.pcol[:], T.part[:], 1.0 / 4096, T.qc[:], Op.mult, Op.add).then_inc(S.vpar, 1)
     V.memset(T.kva[:, 16:32], 0.0).then_inc(S.vkz, 1)
     V.memset(T.kvb[:, 16:32], 0.0).then_inc(S.vkz, 1)
-    V.wait_ge(S.gri, 2)
-    V.tensor_scalar(T.ls[:, 0:8], T.ri[:], T.pmod[:], None, Op.add).then_inc(S.vl, 1)
-    V.tensor_scalar(T.kl[:, 0:4], T.rk[:], T.pmod[:], None, Op.add).then_inc(S.k0, 1)
-    V.wait_ge(S.vc16, 2)
-    V.wait_ge(S.vlists, 2)
-    for b in range(4):
-        c0, c1 = max(4, 32 * b), 32 * b + 32
-        V.wait_ge(S["ev%d" % b], 1)
-        V.tensor_tensor(T.tokx[:, 16 * c0:16 * c1], T.c16[:, 0:16].indirect(T.hi[:, c0:c1]), T.tokrow[:, 16 * c0:16 * c1],
-                        Op.add).then_inc(S.vtx, 1)
+    V.memset(T.ww[:, 2 * MID - ZV * ZC:2 * MID], 0.0).then_inc(S.vzb, 1)
+    V.wait_ge(S.gri, 1)
+    V.tensor_scalar(T.ls[:, 0:4], T.rk[:], T.pmod[:], None, Op.add).then_inc(S.k0, 1)
+    V.wait_ge(S.gwi, 1)
+    V.tensor_scalar(T.tab[:], T.wi[:], T.pmod[:], 0.0, Op.add, Op.is_equal).then_inc(S.vtab, 1)
+    V.wait_ge(S.vlist, 1)
+    V.wait_ge(S.vpar, 2)
+
+    def offs(b):
+        P.matmul(T["tr%d" % b][:, 0:512], T.mrf[:], T.sel[:, 0:512], True, False).then_inc(S["ptr%d" % b], 1)
+
+    def toks(b):
+        for k in range(4):
+            a = 4 * b + k
+            P.matmul(T["tr%d" % b][:, 128 * k:128 * k + 128], T.sel[:, 128 * a:128 * a + 128], T.tokf[:], False,
+                     b > 1 and k == 3).then_inc(S["ptr%d" % b], 1)
+
+    def places(b):
+        P.matmul(T["tr%d" % b][:, 0:512], T.grp[:], T.hx[:, 512 * b:512 * b + 512], b > 1, b < 2).then_inc(S["ptr%d" % b], 1)
 
     P.wait_ge(S.vsel, 16)
+    P.wait_ge(S.vmr, 1)
+    offs(0)
+    offs(1)
     P.wait_ge(S.vtok, 1)
-    for a in range(16):
-        P.matmul(T["tr%d" % (a // 4)][:, 128 * (a % 4):128 * (a % 4) + 128], T.sel[:, 128 * a:128 * a + 128], T.tokf[:],
-                 True, True).then_inc(S["ptr%d" % (a // 4)], 1)
-    P.wait_ge(S.vtab, 16)
-    P.wait_ge(S.vcst, 2)
-    P.wait_ge(S.gpre, 2)
+    toks(0)
+    toks(1)
+    P.wait_ge(S.vgrp, 1)
+    P.wait_ge(S.vhx, HV)
+    P.wait_ge(S.ahx, 16 - HV)
+    places(0)
+    places(1)
+    for b in (2, 3):
+        places(b)
+        toks(b)
+    P.wait_ge(S.vcst, 1)
+    P.wait_ge(S.gpre, 1)
     for c, (c0, c1) in enumerate(CH):
-        ps, sem = T["ps%d" % c], S["pok%d" % c]
-        P.matmul(ps[:, 0:c1 - c0], T.mmod[:], T.cst[:, 0:c1 - c0], True, False).then_inc(sem, 1)
-        P.matmul(ps[:, 0:c1 - c0], T.cst[:], T.c16r[:, c0:c1], False, False).then_inc(sem, 1)
-        if c == last:
-            P.matmul(ps[:, 0:c1 - c0], T.cst[:], T.kst[:, 0:c1 - c0], False, False).then_inc(sem, 1)
+        P.matmul(ps[c][:, 0:c1 - c0], T.cst[:], T.c16r[:, c0:c1], True, False).then_inc(S["pok%d" % c], 1)
+    P.wait_ge(S.vtab, 1)
 
-    def zeros(b, sem):
-        for k in range(4):
-            A.activation(T.ww[:, b + 516 * k:b + 516 * k + 516], T.zero[:], Fn.Silu).then_inc(sem, 1)
+    def zeros(b, k0, k1, sem):
+        for k in range(k0, k1):
+            A.activation(T.ww[:, b + ZC * k:b + ZC * k + ZC], T.zero[:], Fn.Silu).then_inc(sem, 1)
 
+    def row(b):
+        A.wait_ge(S["ptr%d" % b], 6 if b < 2 else 5)
+        A.activation(T.tokx[:, 512 * b:512 * b + 512], T["tr%d" % b][:], Fn.Identity, bias=2048.0 if b < 2 else T.pb[:]).then_inc(
+            S["ev%d" % b], 1)
+
+    A.wait_ge(S.gmb, 1)
+    A.activation(T.ab[:], T.mb[:], Fn.Abs, bias=-7.5).then_inc(S.aab, 1)
     A.wait_ge(S.vz, 1)
-    zeros(NODE, S.afa)
-    for b in range(4):
-        A.wait_ge(S["ptr%d" % b], 4)
-        A.activation(T.tokrow[:, 512 * b:512 * b + 512], T["tr%d" % b][:], Fn.Identity).then_inc(S["ev%d" % b], 1)
-    zeros(MID, S.afb)
+    zeros(NODE, 0, NZ // 2, S.afa)
+    A.wait_ge(S.vmsk, 1)
+    A.wait_ge(S.vhf, 1)
+    for i in range(HV, 16):
+        A.activation(T.hx[:, i:2048:16], T.hif[:], Fn.Copy, scale=T.msk[:, i:i + 1]).then_inc(S.ahx, 1)
+    zeros(NODE, NZ // 2, NZ, S.afa)
+    row(0)
+    row(1)
+    zeros(MID + NODE, 0, NZ // 2, S.afb)
+    A.wait_ge(S.vpb, 1)
+    row(2)
+    row(3)
+    zeros(MID + NODE, NZ // 2, NZ - ZV, S.afb)
 
     V.wait_ge(S.ldown, 16)
-    prev = T.own
-    for k, m in ((1, T.tr1), (2, T.tr0)):
+    prev = T.own[:, 0:128]
+    for k in (1, 2):
+        m = T.pm[:, 128 * k - 128:128 * k]
         V.wait_ge(S["arr%d" % k], ne[k])
-        V.tensor_tensor(m[:, 0:128], prev[:, 0:128], T["land%d" % k][:], Op.max).then_inc(S["vm%d" % k], 1)
+        V.tensor_tensor(m, prev, T["land%d" % k][:], Op.max).then_inc(S["vm%d" % k], 1)
         V.wait_ge(S["vm%d" % k], 1)
         prev = m
     V.wait_ge(S.arr3, ne[3])
     for h in range(2):
-        V.tensor_tensor(T.mx[:, 64 * h:64 * h + 64], prev[:, 64 * h:64 * h + 64], T.land3[:, 64 * h:64 * h + 64],
+        V.tensor_tensor(T.mx[:, 64 * h:64 * h + 64], T.pm[:, 128 + 64 * h:192 + 64 * h], T.land3[:, 64 * h:64 * h + 64],
                         Op.max).then_inc(S["vm3%d" % h], 1)
     for h in range(2):
         V.wait_ge(S["vm3%d" % h], 1)
         V.tensor_scalar(T.tgt[:, 64 * h:64 * h + 64], T.mx[:, 64 * h:64 * h + 64], 4095, None, Op.bitwise_and).then_inc(S.vtgt, 1)
     V.wait_ge(S.vtgt, 2)
-    V.wait_ge(S.vtx, 4)
 
     def match(c):
         c0, c1 = CH[c]
+        for b in range(4):
+            if c0 < 32 * b + 32 and c1 > 32 * b:
+                V.wait_ge(S["ev%d" % b], 1)
         V.tensor_tensor(T.eq[:, 16 * c0:16 * c1], T.tgt[:, 0:128].indirect(T.lo[:, c0:c1]), T.tokx[:, 16 * c0:16 * c1],
-                        Op.not_equal if c == last else Op.is_equal).then_inc(S["veq%d" % c], 1)
+                        Op.is_equal).then_inc(S["veq%d" % c], 1)
         P.wait_ge(S["veq%d" % c], 1)
         for i in range(16):
-            P.matmul(T["ps%d" % c][:, 0:c1 - c0], T.tab[:, 128 * i:128 * i + 128], T.eq[:, 16 * c0 + i:16 * c1:16],
+            P.matmul(ps[c][:, 0:c1 - c0], T.tab[:, 15 - i:143 - i], T.eq[:, 16 * c0 + i:16 * c1:16],
                      False, i == 15).then_inc(S["pok%d" % c], 1)
 
     def offsets(c):
         c0, c1 = CH[c]
-        V.wait_ge(S["pok%d" % c], 19 if c == last else 18)
-        V.tensor_tensor(T.offi[:, c0:c1], T["ps%d" % c][:, 0:c1 - c0], T.pcol[:, c0:c1],
-                        Op.max if c == last else Op.min).then_inc(S["vo%d" % c], 1)
+        V.wait_ge(S["pok%d" % c], 17)
+        V.tensor_tensor(T.offi[:, c0:c1], ps[c][:, 0:c1 - c0], T.pcol[:, c0:c1], Op.min).then_inc(S["vo%d" % c], 1)
         V.wait_ge(S["vo%d" % c], 1)
-        V.tensor_copy(T.off[:, c0:c1], T.offi[:, c0:c1]).then_inc(S["voff%d" % c], 1)
+        V.tensor_scalar(T.off[:, c0:c1], T.offi[:, c0:c1], 4096.0, T.pmod[:], Op.mult, Op.add).then_inc(S["voff%d" % c], 1)
 
     match(0)
-    for c in range(1, last + 1):
-        match(c)
-        offsets(c - 1)
-    offsets(last)
-    A.wait_ge(S.afa, 4)
-    for c in range(last):
+    match(1)
+    offsets(0)
+    match(2)
+    offsets(1)
+    A.wait_ge(S.afa, NZ)
+    for k, c in enumerate((0, 2)):
         c0, c1 = CH[c]
         A.wait_ge(S["gj%d" % c], 1)
         A.wait_ge(S["voff%d" % c], 1)
-        if c:
-            A.wait_ge(S["sc%d" % (c - 1)], 1)
+        if k:
+            A.wait_ge(S.sca0, 1)
         A.activation(T.ww[:, 0:MID].indirect(T.off[:, c0:c1]), T.jrow[:, 16 * c0 - 64:16 * c1 - 64], Fn.Silu).then_inc(
-            S["sc%d" % c], 1)
-    c0, c1 = CH[last]
-    V.wait_ge(S.afb, 4)
-    V.wait_ge(S["gj%d" % last], 1)
-    V.wait_ge(S["voff%d" % last], 1)
-    V.tensor_copy(T.ww[:, MID:2 * MID].indirect(T.off[:, c0:c1]), T.jrow[:, 16 * c0 - 64:16 * c1 - 64]).then_inc(
-        S["sc%d" % last], 1)
-    V.wait_ge(S.vl, 1)
+            S["sca%d" % k], 1)
+    V.wait_ge(S.vzb, 1)
+    V.wait_ge(S.afb, NZ - ZV)
+    V.wait_ge(S.gj1, 1)
+    V.wait_ge(S.voff1, 1)
+    for k, (c0, c1) in enumerate(((CH[1][0], VS), (VS, CH[1][1]))):
+        if k:
+            offsets(2)
+            V.wait_ge(S.scv0, 1)
+        V.tensor_copy(T.ww[:, MID:2 * MID].indirect(T.off[:, c0:c1]), T.jrow[:, 16 * c0 - 64:16 * c1 - 64]).then_inc(
+            S["scv%d" % k], 1)
+    V.wait_ge(S.k0, 1)
+    V.wait_ge(S.vmsk, 1)
     V.wait_ge(S.grst, 1)
-    V.wait_ge(S["sc%d" % (last - 1)], 1)
-    V.wait_ge(S["sc%d" % last], 1)
-
-    def keys_of(d):
-        e0 = 128 * (d - 1)
-        V.tensor_copy(T.kl[:, 4 * d:4 * d + 4], T.ts[:, e0 + 31:e0 + 128:32]).then_inc(S["k%d" % d], 1)
-
+    V.wait_ge(S.sca1, 1)
+    V.wait_ge(S.scv1, 1)
     for d in range(7):
         for h in range(2):
-            e0, b = 128 * d + 64 * h, 8 * d + 4 * h
+            e0, b = 128 * d + 64 * h, 4 * d + 2 * h
             if d:
-                V.wait_ge(S["l%d%d" % (d - 1, h)], 2)
-            V.tensor_tensor(T.vs[:, e0:e0 + 64], T.ww[:, NODE:MID + REG].indirect(T.ls[:, b:b + 4]), T.msk[:], Op.mult).then_inc(
-                S["x%d%d" % (d, h)], 1)
-        if d:
-            keys_of(d)
+                V.wait_ge(S["l%d%d" % (d - 1, h)], 1)
+            for w, w0 in enumerate((NODE, MID + NODE)):
+                V.tensor_tensor(T.vs[:, e0 + w:e0 + 64:2], T.ww[:, w0:w0 + REG].indirect(T.ls[:, b:b + 2]), T.msk[:],
+                                Op.mult).then_inc(S["x%d%d" % (d, h)], 1)
         for h in range(2):
             e0 = 128 * d + 64 * h
-            V.wait_ge(S["x%d%d" % (d, h)], 1)
+            V.wait_ge(S["x%d%d" % (d, h)], 2)
             V.tensor_tensor_scan(T.ts[:, e0:e0 + 64], T.rst[:], T.vs[:, e0:e0 + 64], 0.0, Op.min, Op.add).then_inc(
                 S["t%d%d" % (d, h)], 1)
         for h in range(2):
-            e0, b = 128 * d + 64 * h, 8 * d + 8 + 4 * h
+            e0, b = 128 * d + 64 * h, 4 * d + 4 + 2 * h
             V.wait_ge(S["t%d%d" % (d, h)], 1)
-            if d < 6:
-                V.tensor_copy(T.ls[:, b:b + 4:2], T.ts[:, e0 + 31:e0 + 64:32]).then_inc(S["l%d%d" % (d, h)], 1)
-                V.tensor_scalar(T.ls[:, b + 1:b + 4:2], T.ts[:, e0 + 31:e0 + 64:32], float(REG), None, Op.add).then_inc(
-                    S["l%d%d" % (d, h)], 1)
-    keys_of(7)
+            V.tensor_copy(T.ls[:, b:b + 2], T.ts[:, e0 + 31:e0 + 64:32]).then_inc(S["l%d%d" % (d, h)], 1)
+
+    def list_of(q, d):
+        if d == 0:
+            q.wait_ge(S.k0, 1)
+        else:
+            q.wait_ge(S["l%d0" % (d - 1)], 1)
+            q.wait_ge(S["l%d1" % (d - 1)], 1)
+
     dst = cores[mate]
     rid, pid = topo.addr(dst, core)
     nl = len(topo.engines(core, dst))
     for d in range(1, 6):
-        g.wait_ge(S["k%d" % d], 1)
-    g.remote_dma(T.k2[:, 4:24], T.kl[:, 4:24], S.lst, S.lsent, pid, rid, topo.mask(core, dst))
-    g.wait_ge(S.k6, 1)
-    g.wait_ge(S.k7, 1)
-    g.remote_dma(T.k2[:, 24:32], T.kl[:, 24:32], S.lst2, S.lsent, pid, rid, topo.mask(core, dst))
+        list_of(g, d)
+    g.remote_dma(T.k2[:, 4:24], T.ls[:, 4:24], S.lst, S.lsent, pid, rid, topo.mask(core, dst))
+    for d in (6, 7):
+        list_of(g, d)
+    g.remote_dma(T.k2[:, 24:32], T.ls[:, 24:32], S.lst2, S.lsent, pid, rid, topo.mask(core, dst))
     g.wait_ge(S.lsent, 2 * nl)
     ka, kb = T.kva[:, 16:2065], T.kvb[:, 16:2065]
     A.wait_ge(S.ldkv, 32)
     for d in range(8):
-        A.wait_ge(S["k%d" % d], 1)
-        A.activation(T.ya[:, d:512:8], ka.indirect(T.kl[:, 4 * d:4 * d + 4]), Fn.Copy).then_inc(S.aya, 1)
+        list_of(A, d)
+        A.activation(T.ya[:, d:512:8], ka.indirect(T.ls[:, 4 * d:4 * d + 4]), Fn.Copy).then_inc(S.aya, 1)
     Y.wait_ge(S.aya, 8)
     Y.dma_start(T.y[:, 512 * mine:512 * mine + 512], T.ya[:]).then_inc(S.st1, 16)
     V.wait_ge(S.ldkv, 32)
-    V.wait_ge(S.k0, 1)
-    V.tensor_copy(T.yb[:, 0:512:8], kb.indirect(T.kl[:, 0:4])).then_inc(S.vyb, 1)
+    V.tensor_copy(T.yb[:, 0:512:8], kb.indirect(T.ls[:, 0:4])).then_inc(S.vyb, 1)
     V.wait_ge(S.lst, nl)
     A.wait_ge(S.lst, nl)
     for d in (1, 2):

@@ -1,13 +1,20 @@
 from concourse.mybir import AluOpType as Op, ActivationFunctionType as Fn
 
-CH = [(4, 46), (46, 96), (96, 128)]
-VS = 64
+CH = [(4, 42), (42, 94), (94, 128)]
+VS = 56
 NODE, REG = 2048, 2064
 MID = NODE + REG
 ZC = 258
 NZ = REG // ZC
-ZV = 2
-HV = 12
+Z0 = 4
+ZR = (0, 0, 1, 3, 6)
+ZA = MID + NODE + ZR[4] * ZC
+ZB = 2 * MID - 128
+HV = 13
+SP = {1: slice(0, None, 2), 2: slice(1, None, 2), 3: slice(0, None)}
+W = 2.0 ** 24
+EARLY = 5
+KV1, KV2 = (1, 2), (6,)
 
 I32 = ("sbuf", [128, 128], "int32")
 U16 = ("sbuf", [128, 128], "uint16")
@@ -26,18 +33,18 @@ SCRATCH = {
     "sm": sb(32, "int32"), "d15": sb(32, "int32"), "pmod": sb(1), "pb": sb(1), "qc": sb(1), "mb": B16, "ab": B16, "grp": B16,
     "mcol": sb(16, "bfloat16"), "msk": sb(32), "mr": B16, "mrf": F16, "hx": sb(2048, "bfloat16"),
     "sel": sb(2048, "float16"), "wi": sb(144, "bfloat16"), "tab": sb(144, "float16"), "cst": B16,
-    "c16r": B16, "rst": sb(64), "rk": sb(4, "int32"), "jrow": sb(1984),
+    "c16r": B16, "cc": sb(64), "c1": sb(32), "c2": sb(32), "sc": sb(1), "jrow": sb(1984),
     "tokx": sb(2048), "eq": sb(2048, "float16"), "offi": sb(128), "off": U16, "zero": sb(ZC), "ww": sb(2 * MID),
-    "vs": sb(896, "float16"), "ts": sb(896), "ls": sb(32, "uint16"), "k2": sb(32, "uint16"),
+    "vs": sb(896), "ts": sb(896), "ls": sb(32, "uint16"), "k2": sb(32, "uint16"),
     "kva": sb(2080, "bfloat16"), "kvb": sb(2080, "bfloat16"), "ya": sb(512, "bfloat16"), "yb": sb(512, "bfloat16"),
     "tr0": PS, "tr1": PS, "tr2": PS, "tr3": PS, "ps0": PS, "ps1": PS, "ps2": PS, "pm": PS,
 }
 SEMAPHORES = (["ld1", "ld2", "ld3", "ldown", "ldtok", "ldpar", "ldkv", "sent", "arr1", "arr2", "arr3", "lst", "lst2", "lsent",
-               "st1", "gsm", "gmb", "gmr", "gwi", "gpre", "grst", "gri",
-               "vz", "vzb", "vkz", "vcst", "vsel", "vmr", "vtok", "vpar", "vhi", "vhf", "vhx", "ahx", "vlist", "vpmod", "vpb", "vqc",
-               "vtab", "vd15", "vmsk", "vmcol", "aab", "vgrp", "vm1", "vm2", "vm30", "vm31", "vtgt", "vyb", "aya", "ayb", "k0",
-               "afa", "afb", "ev0", "ev1", "ev2", "ev3", "ptr0", "ptr1", "ptr2", "ptr3", "sca0", "sca1", "scv0", "scv1"]
-              + ["%s%d%d" % (w, d, h) for w in ("x", "t", "l") for d in range(7) for h in range(2)]
+               "st1", "gsm", "gmb", "gmr", "gwi", "gpre", "vc1", "vcc", "vsc",
+               "vz", "vzb", "vkz", "vcst", "vsel", "vmr", "vtok", "vpar", "vpcol", "vhi", "vhf", "vhx", "ahx", "vlist", "vpmod",
+               "vpb", "vqc", "vtab", "vd15", "vmsk", "vmcol", "aab", "vgrp", "vm1", "vm2", "vm30", "vm31", "vtgt", "vyb", "aya",
+               "ayb", "afa", "afb", "ev0", "ev1", "ev2", "ev3", "ptr0", "ptr1", "ptr2", "ptr3", "sca", "scv"]
+              + ["%s%d%d" % (w, d, h) for w in ("x", "y", "t", "l") for d in range(7) for h in range(2)]
               + ["%s%d" % (w, c) for w in ("veq", "pok", "vo", "voff", "gj") for c in range(len(CH))])
 
 
@@ -58,12 +65,13 @@ def rank_program(g, core, T, topo):
         return T.best[:, q * 2048:(q + 1) * 2048]
 
     Y.dma_start(T.snd[:, 0:128], blk((r + 1) % n)).then_inc(S.ld1, 16)
-    A.dma_start(T.tokc[:], T.tok[:]).then_inc(S.ldtok, 16)
-    Y.dma_start(T.part[:], T.par[:]).then_inc(S.ldpar, 16)
+    A.dma_start(T.part[:], T.par[:]).then_inc(S.ldpar, 16)
+    Y.dma_start(T.tokc[:], T.tok[:]).then_inc(S.ldtok, 16)
     A.dma_start(T.snd[:, 128:256], blk((r + 2) % n)).then_inc(S.ld2, 16)
     Y.dma_start(T.snd[:, 256:384], blk((r + 3) % n)).then_inc(S.ld3, 16)
     A.dma_start(T.own[:], blk(r)).then_inc(S.ldown, 16)
-    ne = {k: len(topo.engines(core, cores[(r + k) % n])) for k in (1, 2, 3)}
+    eng = {k: topo.engines(core, cores[(r + k) % n])[SP[k]] for k in (1, 2, 3)}
+    ne = {k: len(eng[k]) for k in eng}
     Y.wait_ge(S.vkz, 2)
     Y.wait_ge(S.sent, sum(ne.values()))
     Y.dma_start(T.kva[:, 17:2065], T.kv[:, mine * 2048:(mine + 1) * 2048]).then_inc(S.ldkv, 16)
@@ -76,13 +84,12 @@ def rank_program(g, core, T, topo):
         dst = cores[(r + k) % n]
         rid, pid = topo.addr(dst, core)
         g.wait_ge(S["ld%d" % k], 16)
-        g.remote_dma(T["land%d" % k][:], T.snd[:, (k - 1) * 128:k * 128], S["arr%d" % k], S.sent, pid, rid, topo.mask(core, dst))
-    g.iota(T.rk[:], [[16, 4]], 1, 0).then_inc(S.gri, 1)
+        g.remote_dma(T["land%d" % k][:], T.snd[:, (k - 1) * 128:k * 128], S["arr%d" % k], S.sent, pid, rid,
+                     sum(1 << e for e in eng[k]))
     g.iota(T.wi[:], [[1, 144]], -15, -1, **low).then_inc(S.gwi, 1)
     g.iota(T.c16r[:], [[16, 128]], 0, 0, **low).then_inc(S.gpre, 1)
     for c, (c0, c1) in enumerate(CH):
         g.iota(T.jrow[:, 16 * c0 - 64:16 * c1 - 64], [[1, 16 * (c1 - c0)]], 16 * c0 + 1, 0, **low).then_inc(S["gj%d" % c], 1)
-    g.iota(T.rst[:], [[0, 2], [3000, 32]], 0, 0, **low).then_inc(S.grst, 1)
 
     V.memset(T.zero[:], 0.0).then_inc(S.vz, 1)
     V.wait_ge(S.gmb, 1)
@@ -99,33 +106,24 @@ def rank_program(g, core, T, topo):
     V.tensor_scalar(T.mcol[:], T.d15[:, 0:16], 0.0, None, Op.is_equal).then_inc(S.vmcol, 1)
     V.tensor_copy(T.pmod[:], T.d15[:, 0:1]).then_inc(S.vpmod, 1)
     V.memset(T.cst[:], 2.0 ** -19).then_inc(S.vcst, 1)
+    V.memset(T.cc[:, 1:64:2], 1.0).then_inc(S.vcc, 1)
+    V.memset(T.kva[:, 16:32], 0.0).then_inc(S.vkz, 1)
+    V.memset(T.kvb[:, 16:32], 0.0).then_inc(S.vkz, 1)
+    V.wait_ge(S.vpmod, 1)
+    V.tensor_scalar(T.pb[:], T.pmod[:], -4096.0, 2048.0, Op.mult, Op.add).then_inc(S.vpb, 1)
+    V.tensor_scalar(T.qc[:], T.pmod[:], -1.0 / 4096, (NODE + 1) / 4096, Op.mult, Op.add).then_inc(S.vqc, 1)
     V.wait_ge(S.ldpar, 16)
     V.tensor_scalar(T.parhi[:], T.part[:], 7, None, Op.arith_shift_right).then_inc(S.vhi, 1)
     V.wait_ge(S.ldtok, 16)
     V.tensor_scalar(T.tokf[:], T.tokc[:], -2048.0, None, Op.add).then_inc(S.vtok, 1)
     V.wait_ge(S.vhi, 1)
     V.tensor_scalar(T.hif[:], T.parhi[:], 2.0, None, Op.mult).then_inc(S.vhf, 1)
-    V.wait_ge(S.vpmod, 1)
-    V.tensor_scalar(T.pb[:], T.pmod[:], -4096.0, 2048.0, Op.mult, Op.add).then_inc(S.vpb, 1)
+    V.tensor_scalar(T.parlo[:], T.part[:], 127, None, Op.bitwise_and).then_inc(S.vpar, 1)
     V.wait_ge(S.vmcol, 1)
     V.wait_ge(S.vhf, 1)
     for i in range(HV):
         V.tensor_scalar(T.hx[:, i:2048:16], T.hif[:], T.mcol[:, i:i + 1], None, Op.mult).then_inc(S.vhx, 1)
-    V.tensor_scalar(T.parlo[:], T.part[:], 127, None, Op.bitwise_and).then_inc(S.vpar, 1)
-    V.tensor_scalar(T.qc[:], T.pmod[:], -1.0 / 4096, (NODE + 1) / 4096, Op.mult, Op.add).then_inc(S.vqc, 1)
-    V.wait_ge(S.vpar, 1)
-    V.tensor_copy(T.lo[:], T.parlo[:]).then_inc(S.vlist, 1)
-    V.wait_ge(S.vqc, 1)
-    V.tensor_scalar(T.pcol[:], T.part[:], 1.0 / 4096, T.qc[:], Op.mult, Op.add).then_inc(S.vpar, 1)
-    V.memset(T.kva[:, 16:32], 0.0).then_inc(S.vkz, 1)
-    V.memset(T.kvb[:, 16:32], 0.0).then_inc(S.vkz, 1)
-    V.memset(T.ww[:, 2 * MID - ZV * ZC:2 * MID], 0.0).then_inc(S.vzb, 1)
-    V.wait_ge(S.gri, 1)
-    V.tensor_scalar(T.ls[:, 0:4], T.rk[:], T.pmod[:], None, Op.add).then_inc(S.k0, 1)
-    V.wait_ge(S.gwi, 1)
-    V.tensor_scalar(T.tab[:], T.wi[:], T.pmod[:], 0.0, Op.add, Op.is_equal).then_inc(S.vtab, 1)
-    V.wait_ge(S.vlist, 1)
-    V.wait_ge(S.vpar, 2)
+    V.memset(T.ww[:, ZA:ZB], 0.0).then_inc(S.vzb, 1)
 
     def offs(b):
         P.matmul(T["tr%d" % b][:, 0:512], T.mrf[:], T.sel[:, 0:512], True, False).then_inc(S["ptr%d" % b], 1)
@@ -164,27 +162,21 @@ def rank_program(g, core, T, topo):
         for k in range(k0, k1):
             A.activation(T.ww[:, b + ZC * k:b + ZC * k + ZC], T.zero[:], Fn.Silu).then_inc(sem, 1)
 
-    def row(b):
-        A.wait_ge(S["ptr%d" % b], 6 if b < 2 else 5)
-        A.activation(T.tokx[:, 512 * b:512 * b + 512], T["tr%d" % b][:], Fn.Identity, bias=2048.0 if b < 2 else T.pb[:]).then_inc(
-            S["ev%d" % b], 1)
-
     A.wait_ge(S.gmb, 1)
     A.activation(T.ab[:], T.mb[:], Fn.Abs, bias=-7.5).then_inc(S.aab, 1)
     A.wait_ge(S.vz, 1)
-    zeros(NODE, 0, NZ // 2, S.afa)
+    zeros(NODE, 0, Z0, S.afa)
     A.wait_ge(S.vmsk, 1)
     A.wait_ge(S.vhf, 1)
     for i in range(HV, 16):
         A.activation(T.hx[:, i:2048:16], T.hif[:], Fn.Copy, scale=T.msk[:, i:i + 1]).then_inc(S.ahx, 1)
-    zeros(NODE, NZ // 2, NZ, S.afa)
-    row(0)
-    row(1)
-    zeros(MID + NODE, 0, NZ // 2, S.afb)
+    zeros(NODE, Z0, NZ, S.afa)
     A.wait_ge(S.vpb, 1)
-    row(2)
-    row(3)
-    zeros(MID + NODE, NZ // 2, NZ - ZV, S.afb)
+    for b in range(4):
+        A.wait_ge(S["ptr%d" % b], 6 if b < 2 else 5)
+        A.activation(T.tokx[:, 512 * b:512 * b + 512], T["tr%d" % b][:], Fn.Identity, bias=2048.0 if b < 2 else T.pb[:]).then_inc(
+            S["ev%d" % b], 1)
+        zeros(MID + NODE, ZR[b], ZR[b + 1], S.afb)
 
     V.wait_ge(S.ldown, 16)
     prev = T.own[:, 0:128]
@@ -192,6 +184,12 @@ def rank_program(g, core, T, topo):
         m = T.pm[:, 128 * k - 128:128 * k]
         V.wait_ge(S["arr%d" % k], ne[k])
         V.tensor_tensor(m, prev, T["land%d" % k][:], Op.max).then_inc(S["vm%d" % k], 1)
+        if k == 1:
+            V.wait_ge(S.gwi, 1)
+            V.tensor_scalar(T.tab[:], T.wi[:], T.pmod[:], 0.0, Op.add, Op.is_equal).then_inc(S.vtab, 1)
+        else:
+            V.wait_ge(S.vpar, 1)
+            V.tensor_copy(T.lo[:], T.parlo[:]).then_inc(S.vlist, 1)
         V.wait_ge(S["vm%d" % k], 1)
         prev = m
     V.wait_ge(S.arr3, ne[3])
@@ -201,6 +199,9 @@ def rank_program(g, core, T, topo):
     for h in range(2):
         V.wait_ge(S["vm3%d" % h], 1)
         V.tensor_scalar(T.tgt[:, 64 * h:64 * h + 64], T.mx[:, 64 * h:64 * h + 64], 4095, None, Op.bitwise_and).then_inc(S.vtgt, 1)
+    V.wait_ge(S.vqc, 1)
+    V.tensor_scalar(T.pcol[:], T.part[:], 1.0 / 4096, T.qc[:], Op.mult, Op.add).then_inc(S.vpcol, 1)
+    V.wait_ge(S.vlist, 1)
     V.wait_ge(S.vtgt, 2)
 
     def match(c):
@@ -217,8 +218,18 @@ def rank_program(g, core, T, topo):
 
     def offsets(c):
         c0, c1 = CH[c]
+        V.wait_ge(S.vpcol, 1)
         V.wait_ge(S["pok%d" % c], 17)
         V.tensor_tensor(T.offi[:, c0:c1], ps[c][:, 0:c1 - c0], T.pcol[:, c0:c1], Op.min).then_inc(S["vo%d" % c], 1)
+        if c == 0:
+            V.tensor_scalar(T.c1[:], T.d15[:], 15.0, W, Op.is_equal, Op.mult).then_inc(S.vc1, 1)
+            V.tensor_scalar(T.c2[:], T.d15[:], 1.0, None, Op.min).then_inc(S.vc1, 1)
+        elif c == 1:
+            V.memset(T.ww[:, ZB:2 * MID], 0.0).then_inc(S.vzb, 1)
+        else:
+            V.tensor_scalar(T.sc[:], T.pmod[:], 15.0, 1.0 / W, Op.is_equal, Op.max).then_inc(S.vsc, 1)
+            V.wait_ge(S.vc1, 2)
+            V.tensor_tensor(T.cc[:, 0:64:2], T.c1[:], T.c2[:], Op.max).then_inc(S.vcc, 1)
         V.wait_ge(S["vo%d" % c], 1)
         V.tensor_scalar(T.off[:, c0:c1], T.offi[:, c0:c1], 4096.0, T.pmod[:], Op.mult, Op.add).then_inc(S["voff%d" % c], 1)
 
@@ -233,79 +244,97 @@ def rank_program(g, core, T, topo):
         A.wait_ge(S["gj%d" % c], 1)
         A.wait_ge(S["voff%d" % c], 1)
         if k:
-            A.wait_ge(S.sca0, 1)
-        A.activation(T.ww[:, 0:MID].indirect(T.off[:, c0:c1]), T.jrow[:, 16 * c0 - 64:16 * c1 - 64], Fn.Silu).then_inc(
-            S["sca%d" % k], 1)
-    V.wait_ge(S.vzb, 1)
-    V.wait_ge(S.afb, NZ - ZV)
+            A.wait_ge(S.sca, 1)
+        A.activation(T.ww[:, 0:MID].indirect(T.off[:, c0:c1]), T.jrow[:, 16 * c0 - 64:16 * c1 - 64], Fn.Silu).then_inc(S.sca, 1)
+    V.wait_ge(S.vzb, 2)
+    V.wait_ge(S.afb, ZR[4])
     V.wait_ge(S.gj1, 1)
     V.wait_ge(S.voff1, 1)
     for k, (c0, c1) in enumerate(((CH[1][0], VS), (VS, CH[1][1]))):
         if k:
             offsets(2)
-            V.wait_ge(S.scv0, 1)
-        V.tensor_copy(T.ww[:, MID:2 * MID].indirect(T.off[:, c0:c1]), T.jrow[:, 16 * c0 - 64:16 * c1 - 64]).then_inc(
-            S["scv%d" % k], 1)
-    V.wait_ge(S.k0, 1)
-    V.wait_ge(S.vmsk, 1)
-    V.wait_ge(S.grst, 1)
-    V.wait_ge(S.sca1, 1)
-    V.wait_ge(S.scv1, 1)
-    for d in range(7):
-        for h in range(2):
+            V.wait_ge(S.scv, 1)
+        V.tensor_copy(T.ww[:, MID:2 * MID].indirect(T.off[:, c0:c1]), T.jrow[:, 16 * c0 - 64:16 * c1 - 64]).then_inc(S.scv, 1)
+
+    def look(q, d, w):
+        w0 = (NODE, MID + NODE)[w]
+        for h in range(2 if d else 1):
             e0, b = 128 * d + 64 * h, 4 * d + 2 * h
             if d:
-                V.wait_ge(S["l%d%d" % (d - 1, h)], 1)
-            for w, w0 in enumerate((NODE, MID + NODE)):
-                V.tensor_tensor(T.vs[:, e0 + w:e0 + 64:2], T.ww[:, w0:w0 + REG].indirect(T.ls[:, b:b + 2]), T.msk[:],
-                                Op.mult).then_inc(S["x%d%d" % (d, h)], 1)
+                q.wait_ge(S["l%d%d" % (d - 1, h)], 1)
+                src, out = T.ww[:, w0:w0 + REG].indirect(T.ls[:, b:b + 2]), T.vs[:, e0 + w:e0 + 64:2]
+            else:
+                src, out = T.ww[:, w0 + 1:w0 + 65], T.vs[:, w:128:2]
+            if w:
+                q.tensor_copy(out, src).then_inc(S["y%d%d" % (d, h)], 1)
+            else:
+                q.activation(out, src, Fn.Copy).then_inc(S["x%d%d" % (d, h)], 1)
+
+    V.wait_ge(S.scv, 2)
+    for d in range(7):
+        look(V, d, 1)
+        if d == 0:
+            V.wait_ge(S.vcc, 2)
+            V.wait_ge(S.vsc, 1)
         for h in range(2):
             e0 = 128 * d + 64 * h
-            V.wait_ge(S["x%d%d" % (d, h)], 2)
-            V.tensor_tensor_scan(T.ts[:, e0:e0 + 64], T.rst[:], T.vs[:, e0:e0 + 64], 0.0, Op.min, Op.add).then_inc(
+            for w in "yx":
+                V.wait_ge(S["%s%d%d" % (w, d, h if d else 0)], 1)
+            V.tensor_tensor_scan(T.ts[:, e0:e0 + 64], T.cc[:], T.vs[:, e0:e0 + 64], 0.0, Op.mult, Op.add).then_inc(
                 S["t%d%d" % (d, h)], 1)
         for h in range(2):
             e0, b = 128 * d + 64 * h, 4 * d + 4 + 2 * h
             V.wait_ge(S["t%d%d" % (d, h)], 1)
-            V.tensor_copy(T.ls[:, b:b + 2], T.ts[:, e0 + 31:e0 + 64:32]).then_inc(S["l%d%d" % (d, h)], 1)
+            V.tensor_scalar(T.ls[:, b:b + 2], T.ts[:, e0 + 31:e0 + 64:32], T.sc[:], 0.25, Op.mult, Op.add).then_inc(
+                S["l%d%d" % (d, h)], 1)
 
     def list_of(q, d):
-        if d == 0:
-            q.wait_ge(S.k0, 1)
-        else:
-            q.wait_ge(S["l%d0" % (d - 1)], 1)
-            q.wait_ge(S["l%d1" % (d - 1)], 1)
+        q.wait_ge(S["l%d0" % (d - 1)], 1)
+        q.wait_ge(S["l%d1" % (d - 1)], 1)
 
     dst = cores[mate]
     rid, pid = topo.addr(dst, core)
     nl = len(topo.engines(core, dst))
-    for d in range(1, 6):
+    m = 4 * EARLY + 4
+    for d in range(1, EARLY + 1):
         list_of(g, d)
-    g.remote_dma(T.k2[:, 4:24], T.ls[:, 4:24], S.lst, S.lsent, pid, rid, topo.mask(core, dst))
-    for d in (6, 7):
+    g.remote_dma(T.k2[:, 4:m], T.ls[:, 4:m], S.lst, S.lsent, pid, rid, topo.mask(core, dst))
+    for d in range(EARLY + 1, 8):
         list_of(g, d)
-    g.remote_dma(T.k2[:, 24:32], T.ls[:, 24:32], S.lst2, S.lsent, pid, rid, topo.mask(core, dst))
+    g.remote_dma(T.k2[:, m:32], T.ls[:, m:32], S.lst2, S.lsent, pid, rid, topo.mask(core, dst))
     g.wait_ge(S.lsent, 2 * nl)
     ka, kb = T.kva[:, 16:2065], T.kvb[:, 16:2065]
-    A.wait_ge(S.ldkv, 32)
+    A.wait_ge(S.sca, 2)
     for d in range(8):
-        list_of(A, d)
-        A.activation(T.ya[:, d:512:8], ka.indirect(T.ls[:, 4 * d:4 * d + 4]), Fn.Copy).then_inc(S.aya, 1)
+        if d < 7:
+            look(A, d, 0)
+        else:
+            list_of(A, d)
+        if d == 0:
+            A.wait_ge(S.ldkv, 32)
+        A.activation(T.ya[:, d:512:8], ka.indirect(T.ls[:, 4 * d:4 * d + 4]) if d else T.kva[:, 17:81], Fn.Copy).then_inc(S.aya, 1)
     Y.wait_ge(S.aya, 8)
     Y.dma_start(T.y[:, 512 * mine:512 * mine + 512], T.ya[:]).then_inc(S.st1, 16)
     V.wait_ge(S.ldkv, 32)
-    V.tensor_copy(T.yb[:, 0:512:8], kb.indirect(T.ls[:, 0:4])).then_inc(S.vyb, 1)
+    V.tensor_copy(T.yb[:, 0:512:8], T.kvb[:, 17:81]).then_inc(S.vyb, 1)
+
+    def keys(d, v):
+        out, src = T.yb[:, d:512:8], kb.indirect(T.k2[:, 4 * d:4 * d + 4])
+        if v:
+            V.tensor_copy(out, src).then_inc(S.vyb, 1)
+        else:
+            A.activation(out, src, Fn.Copy).then_inc(S.ayb, 1)
+
     V.wait_ge(S.lst, nl)
     A.wait_ge(S.lst, nl)
-    for d in (1, 2):
-        V.tensor_copy(T.yb[:, d:512:8], kb.indirect(T.k2[:, 4 * d:4 * d + 4])).then_inc(S.vyb, 1)
-    for d in (3, 4, 5):
-        A.activation(T.yb[:, d:512:8], kb.indirect(T.k2[:, 4 * d:4 * d + 4]), Fn.Copy).then_inc(S.ayb, 1)
+    for d in range(1, EARLY + 1):
+        keys(d, d in KV1)
     V.wait_ge(S.lst2, nl)
     A.wait_ge(S.lst2, nl)
-    V.tensor_copy(T.yb[:, 6:512:8], kb.indirect(T.k2[:, 24:28])).then_inc(S.vyb, 1)
-    A.activation(T.yb[:, 7:512:8], kb.indirect(T.k2[:, 28:32]), Fn.Copy).then_inc(S.ayb, 1)
-    Y.wait_ge(S.vyb, 4)
-    Y.wait_ge(S.ayb, 4)
+    for d in range(EARLY + 1, 8):
+        keys(d, d in KV2)
+    nk = 1 + len(KV1) + len(KV2)
+    Y.wait_ge(S.vyb, nk)
+    Y.wait_ge(S.ayb, 8 - nk)
     Y.dma_start(T.y[:, 512 * other:512 * other + 512], T.yb[:]).then_inc(S.st1, 16)
     Y.wait_ge(S.st1, 32)

from concourse.mybir import AluOpType as Op, ActivationFunctionType as Fn

CH = [(4, 42), (42, 94), (94, 128)]
VS = 56
NODE, REG = 2048, 2064
MID = NODE + REG
ZC = 258
NZ = REG // ZC
Z0 = 4
ZR = (0, 0, 1, 3, 6)
ZA = MID + NODE + ZR[4] * ZC
ZB = 2 * MID - 128
HV = 13
SP = {1: slice(0, None, 2), 2: slice(1, None, 2), 3: slice(0, None)}
W = 2.0 ** 24
EARLY = 5
KV1, KV2 = (1, 2), (6,)

I32 = ("sbuf", [128, 128], "int32")
U16 = ("sbuf", [128, 128], "uint16")
B16 = ("sbuf", [128, 128], "bfloat16")
F16 = ("sbuf", [128, 128], "float16")
PS = ("psum", [128, 512], "float32")


def sb(k, d="float32"):
    return ("sbuf", [128, k], d)


SCRATCH = {
    "own": I32, "snd": sb(384, "int32"), "land1": I32, "land2": I32, "land3": I32, "mx": I32, "tgt": I32,
    "tokc": I32, "tokf": F16, "part": I32, "parlo": I32, "parhi": I32, "lo": U16, "hif": B16, "pcol": sb(128),
    "sm": sb(32, "int32"), "d15": sb(32, "int32"), "pmod": sb(1), "pb": sb(1), "qc": sb(1), "mb": B16, "ab": B16, "grp": B16,
    "mcol": sb(16, "bfloat16"), "msk": sb(32), "mr": B16, "mrf": F16, "hx": sb(2048, "bfloat16"),
    "sel": sb(2048, "float16"), "wi": sb(144, "bfloat16"), "tab": sb(144, "float16"), "cst": B16,
    "c16r": B16, "cc": sb(64), "c1": sb(32), "c2": sb(32), "sc": sb(1), "jrow": sb(1984),
    "tokx": sb(2048), "eq": sb(2048, "float16"), "offi": sb(128), "off": U16, "zero": sb(ZC), "ww": sb(2 * MID),
    "vs": sb(896), "ts": sb(896), "ls": sb(32, "uint16"), "k2": sb(32, "uint16"),
    "kva": sb(2080, "bfloat16"), "kvb": sb(2080, "bfloat16"), "ya": sb(512, "bfloat16"), "yb": sb(512, "bfloat16"),
    "tr0": PS, "tr1": PS, "tr2": PS, "tr3": PS, "ps0": PS, "ps1": PS, "ps2": PS, "pm": PS,
}
SEMAPHORES = (["ld1", "ld2", "ld3", "ldown", "ldtok", "ldpar", "ldkv", "sent", "arr1", "arr2", "arr3", "lst", "lst2", "lsent",
               "st1", "gsm", "gmb", "gmr", "gwi", "gpre", "vc1", "vcc", "vsc",
               "vz", "vzb", "vkz", "vcst", "vsel", "vmr", "vtok", "vpar", "vpcol", "vhi", "vhf", "vhx", "ahx", "vlist", "vpmod",
               "vpb", "vqc", "vtab", "vd15", "vmsk", "vmcol", "aab", "vgrp", "vm1", "vm2", "vm30", "vm31", "vtgt", "vyb", "aya",
               "ayb", "afa", "afb", "ev0", "ev1", "ev2", "ev3", "ptr0", "ptr1", "ptr2", "ptr3", "sca", "scv"]
              + ["%s%d%d" % (w, d, h) for w in ("x", "y", "t", "l") for d in range(7) for h in range(2)]
              + ["%s%d" % (w, c) for w in ("veq", "pok", "vo", "voff", "gj") for c in range(len(CH))])


def rank_program(g, core, T, topo):
    r = T.rank_of(core)
    if r is None:
        return
    S = T.sem
    cores = T.cores
    n = len(cores)
    V, A, P, Y = g.vector, g.scalar, g.tensor, g.sync
    mate = (r + 2) % n
    mine, other = r // 2, 1 - r // 2
    low = {"allow_small_or_imprecise_dtypes": True}
    ps = [T.ps0, T.ps1, T.ps2]

    def blk(q):
        return T.best[:, q * 2048:(q + 1) * 2048]

    Y.dma_start(T.snd[:, 0:128], blk((r + 1) % n)).then_inc(S.ld1, 16)
    A.dma_start(T.part[:], T.par[:]).then_inc(S.ldpar, 16)
    Y.dma_start(T.tokc[:], T.tok[:]).then_inc(S.ldtok, 16)
    A.dma_start(T.snd[:, 128:256], blk((r + 2) % n)).then_inc(S.ld2, 16)
    Y.dma_start(T.snd[:, 256:384], blk((r + 3) % n)).then_inc(S.ld3, 16)
    A.dma_start(T.own[:], blk(r)).then_inc(S.ldown, 16)
    eng = {k: topo.engines(core, cores[(r + k) % n])[SP[k]] for k in (1, 2, 3)}
    ne = {k: len(eng[k]) for k in eng}
    Y.wait_ge(S.vkz, 2)
    Y.wait_ge(S.sent, sum(ne.values()))
    Y.dma_start(T.kva[:, 17:2065], T.kv[:, mine * 2048:(mine + 1) * 2048]).then_inc(S.ldkv, 16)
    Y.dma_start(T.kvb[:, 17:2065], T.kv[:, other * 2048:(other + 1) * 2048]).then_inc(S.ldkv, 16)

    g.iota(T.mb[:], [[-16, 8], [0, 16]], 0, 1, **low).then_inc(S.gmb, 1)
    g.iota(T.sm[:], [[-1, 32]], 0, 1).then_inc(S.gsm, 1)
    g.iota(T.mr[:], [[0, 8], [-4096, 16]], 0, 0, **low).then_inc(S.gmr, 1)
    for k in (1, 2, 3):
        dst = cores[(r + k) % n]
        rid, pid = topo.addr(dst, core)
        g.wait_ge(S["ld%d" % k], 16)
        g.remote_dma(T["land%d" % k][:], T.snd[:, (k - 1) * 128:k * 128], S["arr%d" % k], S.sent, pid, rid,
                     sum(1 << e for e in eng[k]))
    g.iota(T.wi[:], [[1, 144]], -15, -1, **low).then_inc(S.gwi, 1)
    g.iota(T.c16r[:], [[16, 128]], 0, 0, **low).then_inc(S.gpre, 1)
    for c, (c0, c1) in enumerate(CH):
        g.iota(T.jrow[:, 16 * c0 - 64:16 * c1 - 64], [[1, 16 * (c1 - c0)]], 16 * c0 + 1, 0, **low).then_inc(S["gj%d" % c], 1)

    V.memset(T.zero[:], 0.0).then_inc(S.vz, 1)
    V.wait_ge(S.gmb, 1)
    for a in range(16):
        V.tensor_scalar(T.sel[:, 128 * a:128 * a + 128], T.mb[:], float(a), None, Op.is_equal).then_inc(S.vsel, 1)
    V.wait_ge(S.gsm, 1)
    V.tensor_scalar(T.d15[:], T.sm[:], 15, None, Op.bitwise_and).then_inc(S.vd15, 1)
    V.wait_ge(S.gmr, 1)
    V.tensor_copy(T.mrf[:], T.mr[:]).then_inc(S.vmr, 1)
    V.wait_ge(S.aab, 1)
    V.tensor_scalar(T.grp[:], T.ab[:], 8.0, 2048.0, Op.is_lt, Op.mult).then_inc(S.vgrp, 1)
    V.wait_ge(S.vd15, 1)
    V.tensor_scalar(T.msk[:], T.d15[:], 0.0, None, Op.is_equal).then_inc(S.vmsk, 1)
    V.tensor_scalar(T.mcol[:], T.d15[:, 0:16], 0.0, None, Op.is_equal).then_inc(S.vmcol, 1)
    V.tensor_copy(T.pmod[:], T.d15[:, 0:1]).then_inc(S.vpmod, 1)
    V.memset(T.cst[:], 2.0 ** -19).then_inc(S.vcst, 1)
    V.memset(T.cc[:, 1:64:2], 1.0).then_inc(S.vcc, 1)
    V.memset(T.kva[:, 16:32], 0.0).then_inc(S.vkz, 1)
    V.memset(T.kvb[:, 16:32], 0.0).then_inc(S.vkz, 1)
    V.wait_ge(S.vpmod, 1)
    V.tensor_scalar(T.pb[:], T.pmod[:], -4096.0, 2048.0, Op.mult, Op.add).then_inc(S.vpb, 1)
    V.tensor_scalar(T.qc[:], T.pmod[:], -1.0 / 4096, (NODE + 1) / 4096, Op.mult, Op.add).then_inc(S.vqc, 1)
    V.wait_ge(S.ldpar, 16)
    V.tensor_scalar(T.parhi[:], T.part[:], 7, None, Op.arith_shift_right).then_inc(S.vhi, 1)
    V.wait_ge(S.ldtok, 16)
    V.tensor_scalar(T.tokf[:], T.tokc[:], -2048.0, None, Op.add).then_inc(S.vtok, 1)
    V.wait_ge(S.vhi, 1)
    V.tensor_scalar(T.hif[:], T.parhi[:], 2.0, None, Op.mult).then_inc(S.vhf, 1)
    V.tensor_scalar(T.parlo[:], T.part[:], 127, None, Op.bitwise_and).then_inc(S.vpar, 1)
    V.wait_ge(S.vmcol, 1)
    V.wait_ge(S.vhf, 1)
    for i in range(HV):
        V.tensor_scalar(T.hx[:, i:2048:16], T.hif[:], T.mcol[:, i:i + 1], None, Op.mult).then_inc(S.vhx, 1)
    V.memset(T.ww[:, ZA:ZB], 0.0).then_inc(S.vzb, 1)

    def offs(b):
        P.matmul(T["tr%d" % b][:, 0:512], T.mrf[:], T.sel[:, 0:512], True, False).then_inc(S["ptr%d" % b], 1)

    def toks(b):
        for k in range(4):
            a = 4 * b + k
            P.matmul(T["tr%d" % b][:, 128 * k:128 * k + 128], T.sel[:, 128 * a:128 * a + 128], T.tokf[:], False,
                     b > 1 and k == 3).then_inc(S["ptr%d" % b], 1)

    def places(b):
        P.matmul(T["tr%d" % b][:, 0:512], T.grp[:], T.hx[:, 512 * b:512 * b + 512], b > 1, b < 2).then_inc(S["ptr%d" % b], 1)

    P.wait_ge(S.vsel, 16)
    P.wait_ge(S.vmr, 1)
    offs(0)
    offs(1)
    P.wait_ge(S.vtok, 1)
    toks(0)
    toks(1)
    P.wait_ge(S.vgrp, 1)
    P.wait_ge(S.vhx, HV)
    P.wait_ge(S.ahx, 16 - HV)
    places(0)
    places(1)
    for b in (2, 3):
        places(b)
        toks(b)
    P.wait_ge(S.vcst, 1)
    P.wait_ge(S.gpre, 1)
    for c, (c0, c1) in enumerate(CH):
        P.matmul(ps[c][:, 0:c1 - c0], T.cst[:], T.c16r[:, c0:c1], True, False).then_inc(S["pok%d" % c], 1)
    P.wait_ge(S.vtab, 1)

    def zeros(b, k0, k1, sem):
        for k in range(k0, k1):
            A.activation(T.ww[:, b + ZC * k:b + ZC * k + ZC], T.zero[:], Fn.Silu).then_inc(sem, 1)

    A.wait_ge(S.gmb, 1)
    A.activation(T.ab[:], T.mb[:], Fn.Abs, bias=-7.5).then_inc(S.aab, 1)
    A.wait_ge(S.vz, 1)
    zeros(NODE, 0, Z0, S.afa)
    A.wait_ge(S.vmsk, 1)
    A.wait_ge(S.vhf, 1)
    for i in range(HV, 16):
        A.activation(T.hx[:, i:2048:16], T.hif[:], Fn.Copy, scale=T.msk[:, i:i + 1]).then_inc(S.ahx, 1)
    zeros(NODE, Z0, NZ, S.afa)
    A.wait_ge(S.vpb, 1)
    for b in range(4):
        A.wait_ge(S["ptr%d" % b], 6 if b < 2 else 5)
        A.activation(T.tokx[:, 512 * b:512 * b + 512], T["tr%d" % b][:], Fn.Identity, bias=2048.0 if b < 2 else T.pb[:]).then_inc(
            S["ev%d" % b], 1)
        zeros(MID + NODE, ZR[b], ZR[b + 1], S.afb)

    V.wait_ge(S.ldown, 16)
    prev = T.own[:, 0:128]
    for k in (1, 2):
        m = T.pm[:, 128 * k - 128:128 * k]
        V.wait_ge(S["arr%d" % k], ne[k])
        V.tensor_tensor(m, prev, T["land%d" % k][:], Op.max).then_inc(S["vm%d" % k], 1)
        if k == 1:
            V.wait_ge(S.gwi, 1)
            V.tensor_scalar(T.tab[:], T.wi[:], T.pmod[:], 0.0, Op.add, Op.is_equal).then_inc(S.vtab, 1)
        else:
            V.wait_ge(S.vpar, 1)
            V.tensor_copy(T.lo[:], T.parlo[:]).then_inc(S.vlist, 1)
        V.wait_ge(S["vm%d" % k], 1)
        prev = m
    V.wait_ge(S.arr3, ne[3])
    for h in range(2):
        V.tensor_tensor(T.mx[:, 64 * h:64 * h + 64], T.pm[:, 128 + 64 * h:192 + 64 * h], T.land3[:, 64 * h:64 * h + 64],
                        Op.max).then_inc(S["vm3%d" % h], 1)
    for h in range(2):
        V.wait_ge(S["vm3%d" % h], 1)
        V.tensor_scalar(T.tgt[:, 64 * h:64 * h + 64], T.mx[:, 64 * h:64 * h + 64], 4095, None, Op.bitwise_and).then_inc(S.vtgt, 1)
    V.wait_ge(S.vqc, 1)
    V.tensor_scalar(T.pcol[:], T.part[:], 1.0 / 4096, T.qc[:], Op.mult, Op.add).then_inc(S.vpcol, 1)
    V.wait_ge(S.vlist, 1)
    V.wait_ge(S.vtgt, 2)

    def match(c):
        c0, c1 = CH[c]
        for b in range(4):
            if c0 < 32 * b + 32 and c1 > 32 * b:
                V.wait_ge(S["ev%d" % b], 1)
        V.tensor_tensor(T.eq[:, 16 * c0:16 * c1], T.tgt[:, 0:128].indirect(T.lo[:, c0:c1]), T.tokx[:, 16 * c0:16 * c1],
                        Op.is_equal).then_inc(S["veq%d" % c], 1)
        P.wait_ge(S["veq%d" % c], 1)
        for i in range(16):
            P.matmul(ps[c][:, 0:c1 - c0], T.tab[:, 15 - i:143 - i], T.eq[:, 16 * c0 + i:16 * c1:16],
                     False, i == 15).then_inc(S["pok%d" % c], 1)

    def offsets(c):
        c0, c1 = CH[c]
        V.wait_ge(S.vpcol, 1)
        V.wait_ge(S["pok%d" % c], 17)
        V.tensor_tensor(T.offi[:, c0:c1], ps[c][:, 0:c1 - c0], T.pcol[:, c0:c1], Op.min).then_inc(S["vo%d" % c], 1)
        if c == 0:
            V.tensor_scalar(T.c1[:], T.d15[:], 15.0, W, Op.is_equal, Op.mult).then_inc(S.vc1, 1)
            V.tensor_scalar(T.c2[:], T.d15[:], 1.0, None, Op.min).then_inc(S.vc1, 1)
        elif c == 1:
            V.memset(T.ww[:, ZB:2 * MID], 0.0).then_inc(S.vzb, 1)
        else:
            V.tensor_scalar(T.sc[:], T.pmod[:], 15.0, 1.0 / W, Op.is_equal, Op.max).then_inc(S.vsc, 1)
            V.wait_ge(S.vc1, 2)
            V.tensor_tensor(T.cc[:, 0:64:2], T.c1[:], T.c2[:], Op.max).then_inc(S.vcc, 1)
        V.wait_ge(S["vo%d" % c], 1)
        V.tensor_scalar(T.off[:, c0:c1], T.offi[:, c0:c1], 4096.0, T.pmod[:], Op.mult, Op.add).then_inc(S["voff%d" % c], 1)

    match(0)
    match(1)
    offsets(0)
    match(2)
    offsets(1)
    A.wait_ge(S.afa, NZ)
    for k, c in enumerate((0, 2)):
        c0, c1 = CH[c]
        A.wait_ge(S["gj%d" % c], 1)
        A.wait_ge(S["voff%d" % c], 1)
        if k:
            A.wait_ge(S.sca, 1)
        A.activation(T.ww[:, 0:MID].indirect(T.off[:, c0:c1]), T.jrow[:, 16 * c0 - 64:16 * c1 - 64], Fn.Silu).then_inc(S.sca, 1)
    V.wait_ge(S.vzb, 2)
    V.wait_ge(S.afb, ZR[4])
    V.wait_ge(S.gj1, 1)
    V.wait_ge(S.voff1, 1)
    for k, (c0, c1) in enumerate(((CH[1][0], VS), (VS, CH[1][1]))):
        if k:
            offsets(2)
            V.wait_ge(S.scv, 1)
        V.tensor_copy(T.ww[:, MID:2 * MID].indirect(T.off[:, c0:c1]), T.jrow[:, 16 * c0 - 64:16 * c1 - 64]).then_inc(S.scv, 1)

    def look(q, d, w):
        w0 = (NODE, MID + NODE)[w]
        for h in range(2 if d else 1):
            e0, b = 128 * d + 64 * h, 4 * d + 2 * h
            if d:
                q.wait_ge(S["l%d%d" % (d - 1, h)], 1)
                src, out = T.ww[:, w0:w0 + REG].indirect(T.ls[:, b:b + 2]), T.vs[:, e0 + w:e0 + 64:2]
            else:
                src, out = T.ww[:, w0 + 1:w0 + 65], T.vs[:, w:128:2]
            if w:
                q.tensor_copy(out, src).then_inc(S["y%d%d" % (d, h)], 1)
            else:
                q.activation(out, src, Fn.Copy).then_inc(S["x%d%d" % (d, h)], 1)

    V.wait_ge(S.scv, 2)
    for d in range(7):
        look(V, d, 1)
        if d == 0:
            V.wait_ge(S.vcc, 2)
            V.wait_ge(S.vsc, 1)
        for h in range(2):
            e0 = 128 * d + 64 * h
            for w in "yx":
                V.wait_ge(S["%s%d%d" % (w, d, h if d else 0)], 1)
            V.tensor_tensor_scan(T.ts[:, e0:e0 + 64], T.cc[:], T.vs[:, e0:e0 + 64], 0.0, Op.mult, Op.add).then_inc(
                S["t%d%d" % (d, h)], 1)
        for h in range(2):
            e0, b = 128 * d + 64 * h, 4 * d + 4 + 2 * h
            V.wait_ge(S["t%d%d" % (d, h)], 1)
            V.tensor_scalar(T.ls[:, b:b + 2], T.ts[:, e0 + 31:e0 + 64:32], T.sc[:], 0.25, Op.mult, Op.add).then_inc(
                S["l%d%d" % (d, h)], 1)

    def list_of(q, d):
        q.wait_ge(S["l%d0" % (d - 1)], 1)
        q.wait_ge(S["l%d1" % (d - 1)], 1)

    dst = cores[mate]
    rid, pid = topo.addr(dst, core)
    nl = len(topo.engines(core, dst))
    m = 4 * EARLY + 4
    for d in range(1, EARLY + 1):
        list_of(g, d)
    g.remote_dma(T.k2[:, 4:m], T.ls[:, 4:m], S.lst, S.lsent, pid, rid, topo.mask(core, dst))
    for d in range(EARLY + 1, 8):
        list_of(g, d)
    g.remote_dma(T.k2[:, m:32], T.ls[:, m:32], S.lst2, S.lsent, pid, rid, topo.mask(core, dst))
    g.wait_ge(S.lsent, 2 * nl)
    ka, kb = T.kva[:, 16:2065], T.kvb[:, 16:2065]
    A.wait_ge(S.sca, 2)
    for d in range(8):
        if d < 7:
            look(A, d, 0)
        else:
            list_of(A, d)
        if d == 0:
            A.wait_ge(S.ldkv, 32)
        A.activation(T.ya[:, d:512:8], ka.indirect(T.ls[:, 4 * d:4 * d + 4]) if d else T.kva[:, 17:81], Fn.Copy).then_inc(S.aya, 1)
    Y.wait_ge(S.aya, 8)
    Y.dma_start(T.y[:, 512 * mine:512 * mine + 512], T.ya[:]).then_inc(S.st1, 16)
    V.wait_ge(S.ldkv, 32)
    V.tensor_copy(T.yb[:, 0:512:8], T.kvb[:, 17:81]).then_inc(S.vyb, 1)

    def keys(d, v):
        out, src = T.yb[:, d:512:8], kb.indirect(T.k2[:, 4 * d:4 * d + 4])
        if v:
            V.tensor_copy(out, src).then_inc(S.vyb, 1)
        else:
            A.activation(out, src, Fn.Copy).then_inc(S.ayb, 1)

    V.wait_ge(S.lst, nl)
    A.wait_ge(S.lst, nl)
    for d in range(1, EARLY + 1):
        keys(d, d in KV1)
    V.wait_ge(S.lst2, nl)
    A.wait_ge(S.lst2, nl)
    for d in range(EARLY + 1, 8):
        keys(d, d in KV2)
    nk = 1 + len(KV1) + len(KV2)
    Y.wait_ge(S.vyb, nk)
    Y.wait_ge(S.ayb, 8 - nk)
    Y.dma_start(T.y[:, 512 * other:512 * other + 512], T.yb[:]).then_inc(S.st1, 16)
    Y.wait_ge(S.st1, 32)
